import numpy as np
import ml_dtypes


def mxq(x, axis, fmt="e4m3"):
    dtype, down = {"e4m3": (ml_dtypes.float8_e4m3fn, 7), "e5m2": (ml_dtypes.float8_e5m2, 14)}[fmt]
    v = np.moveaxis(np.asarray(x, np.float32).astype(ml_dtypes.bfloat16).astype(np.float64), axis, -1)
    blocks = v.reshape(v.shape[:-1] + (-1, 32))
    amax = np.abs(blocks).max(-1, keepdims=True)
    byte = np.maximum(np.where(amax > 0, np.frexp(amax)[1] - 1 + 127, 0) - down, 1)
    scale = np.exp2(byte - 127.0)
    codes = (blocks / scale).astype(np.float32).astype(dtype).astype(np.float64)
    return np.moveaxis((codes * scale).reshape(v.shape), -1, axis)


WIDE = False


def mx_kscale(k):
    if not WIDE:
        return np.ones(k)
    levels = np.array([10, -10, 5, -5, 0])
    if k % 512:
        return np.exp2(np.random.permutation(np.resize(levels, k // 32))).repeat(32)
    a = np.empty((k // 512, 16))
    for p in range(k // 512):
        a[p, :8] = np.random.permutation(np.resize(levels, 8))
        for g in range(8):
            far = levels[np.abs(levels - a[p, g]) >= 10]
            a[p, g + 8] = far[np.random.randint(len(far))]
    return np.exp2(a.ravel()).repeat(32)


def f64(x):
    return np.asarray(x).astype(np.float64)


def striped(idx):
    return np.tile(idx.reshape(-1, 16).T, (8, 1)).astype(np.uint16)


def unstriped(offs):
    return offs[:16].T.reshape(-1).astype(np.int64)


E2M1 = np.array([0.0, 0.5, 1.0, 1.5, 2.0, 3.0, 4.0, 6.0, -0.0, -0.5, -1.0, -1.5, -2.0, -3.0, -4.0, -6.0])


def pack_weight(w, fmt):
    k, n = w.shape
    w = f64(np.asarray(w, np.float32).astype(ml_dtypes.bfloat16)).reshape(k // 32, 32, n)
    amax = np.abs(w).max(1)
    if fmt == "e4m3":
        byte = np.frexp(amax)[1] - 1 + 127 - 7
    else:
        mant, ex = np.frexp(amax / 6.0)
        byte = np.where(mant > 0.5, ex, ex - 1) + 127
    byte = np.clip(np.where(amax > 0, byte, 1), 1, 254)
    scaled = (w * np.exp2(127.0 - byte)[:, None, :]).reshape(k, n).astype(np.float32)
    by_word = np.ascontiguousarray(scaled.reshape(k // 512, 128, 4, n).transpose(0, 1, 3, 2))
    if fmt == "e4m3":
        words = by_word.astype(ml_dtypes.float8_e4m3fn).view(np.uint8)
    else:
        c = by_word.astype(ml_dtypes.float4_e2m1fn).view(np.uint8) & 0xF
        words = (c[..., 0::2] | (c[..., 1::2] << 4)).reshape(k // 512, 128, 2 * n)
    return np.ascontiguousarray(words), np.ascontiguousarray(byte.astype(np.uint8).reshape(k // 512, 16, n))


def unpack_weight(words, scales, fmt):
    g, _, n = scales.shape
    words = np.ascontiguousarray(words).reshape(g, 128, n, -1)
    if fmt == "e4m3":
        vals = words.view(ml_dtypes.float8_e4m3fn).astype(np.float64)
    else:
        nib = np.empty((g, 128, n, 4), np.uint8)
        nib[..., 0::2] = words & 0xF
        nib[..., 1::2] = words >> 4
        vals = E2M1[nib]
    vals = vals * np.repeat(np.exp2(scales.astype(np.float64) - 127.0), 8, axis=1)[..., None]
    return vals.transpose(0, 1, 3, 2).reshape(g * 512, n)


def relu2(v):
    return np.maximum(v, 0.0) ** 2


K, T, E, C, H, N, HOT = 1536, 1280, 10, 128, 512, 128, 2


def by_expert(wq, xq):
    return np.concatenate([wq[e].T @ xq[:, e * C:(e + 1) * C] for e in range(E)], axis=1)


def setup_inputs():
    n = np.random.standard_normal
    s = mx_kscale(K)
    u = mx_kscale(H)
    slot_token = np.random.permutation(T)[:E * C]
    x = pack_weight(n((K, T)) * s[:, None], "e4m3")
    w1h = [pack_weight(m, "e4m3") for m in n((HOT, K, H)) / np.sqrt(K) / s[None, :, None] * u]
    w2h = [pack_weight(m, "e4m3") for m in n((HOT, H, N)) / np.sqrt(H) / u[None, :, None] ** 2]
    w1c = [pack_weight(m, "e2m1") for m in n((E - HOT, K, H)) / np.sqrt(K) / s[None, :, None] * u]
    w2c = [pack_weight(m, "e2m1") for m in n((E - HOT, H, N)) / np.sqrt(H) / u[None, :, None] ** 2]
    return {
        "x_words": x[0],
        "x_scales": x[1],
        "w1h_words": np.stack([m[0] for m in w1h]),
        "w1h_scales": np.stack([m[1] for m in w1h]),
        "w2h_words": np.stack([m[0] for m in w2h]),
        "w2h_scales": np.stack([m[1] for m in w2h]),
        "w1c_words": np.stack([m[0] for m in w1c]),
        "w1c_scales": np.stack([m[1] for m in w1c]),
        "w2c_words": np.stack([m[0] for m in w2c]),
        "w2c_scales": np.stack([m[1] for m in w2c]),
        "gate": np.tile(np.random.uniform(0.2, 1.0, E * C), (128, 1)).astype(np.float32),
        "offs": striped(slot_token),
    }


def reference(x_words, x_scales, w1h_words, w1h_scales, w2h_words, w2h_scales, w1c_words, w1c_scales, w2c_words, w2c_scales, gate, offs):
    w1h = np.stack([unpack_weight(w1h_words[e], w1h_scales[e], "e4m3") for e in range(HOT)])
    w2h = np.stack([unpack_weight(w2h_words[e], w2h_scales[e], "e4m3") for e in range(HOT)])
    w1c = np.stack([unpack_weight(w1c_words[e], w1c_scales[e], "e2m1") for e in range(E - HOT)])
    w2c = np.stack([unpack_weight(w2c_words[e], w2c_scales[e], "e2m1") for e in range(E - HOT)])
    idx = unstriped(offs)
    xq = unpack_weight(x_words, x_scales, "e4m3")[:, idx]
    w1 = [*w1h, *w1c]
    w2 = [*w2h, *w2c]
    h = relu2(by_expert(w1, xq))
    y = by_expert(w2, mxq(h, 0, "e4m3"))
    out = np.zeros((N, T))
    out[:, idx] = f64(gate[:1]) * y
    return out

@@ -1,0 +1,176 @@
+from contextlib import ExitStack
+
+import concourse.mybir as mybir
+from concourse.masks import make_identity
+
+K, T, E, C, H, N, HOT = 1536, 1280, 10, 128, 512, 128, 2
+COLD = E - HOT
+FLOPS = 2 * E * C * (K * H + H * N)
+
+F32 = mybir.dt.float32
+BF16 = mybir.dt.bfloat16
+I32 = mybir.dt.int32
+U32 = mybir.dt.uint32
+U16 = mybir.dt.uint16
+U8 = mybir.dt.uint8
+FP8X4 = mybir.dt.float8_e4m3fn_x4
+FP4X4 = mybir.dt.float4_e2m1fn_x4
+ACT = mybir.ActivationFunctionType
+MULT = mybir.AluOpType.mult
+
+P = 128
+PACK = 4
+PASSES = K // (P * PACK)
+LIST = 16
+SCALE_WINDOW = 1408
+SHIFT_ROWS = 112
+
+ORDER = [9, 8, 7, 6, 5, 4, 3, 2, 1, 0]
+GATHER = 256
+SCATTERS = {8: (1120, 1280), 7: (960, 1120), 6: (800, 960), 5: (640, 800), 3: (480, 640), 2: (320, 480), 1: (160, 320), 0: (0, 160)}
+
+
+def tile_moe_hot_mlp_relu2_kernel(
+    tc, x_words, x_scales, w1h_words, w1h_scales, w2h_words, w2h_scales,
+    w1c_words, w1c_scales, w2c_words, w2c_scales, gate, offs, out,
+):
+    nc = tc.nc
+    with ExitStack() as ctx:
+        keep = ctx.enter_context(tc.tile_pool(name="keep", bufs=1))
+        ring = ctx.enter_context(tc.tile_pool(name="ring", bufs=4))
+        tokens = ctx.enter_context(tc.tile_pool(name="tokens", bufs=5))
+        psum_h = ctx.enter_context(tc.psum_pool(name="psum_h", bufs=3))
+        psum_t = ctx.enter_context(tc.psum_pool(name="psum_t", bufs=3))
+        psum_y = ctx.enter_context(tc.psum_pool(name="psum_y", bufs=2))
+
+        def held(shape, dtype, name):
+            return keep.tile(shape, dtype, name=name, align_bytes=64)
+
+        offsets = keep.tile([P, T // LIST], U16, name="offsets")
+        xw = [held([P, T], I32, f"xw{s}") for s in range(PASSES)]
+        xs = held([P, SCALE_WINDOW], U8, "xs")
+        w1hs = held([P, HOT * PASSES, H], U8, "w1hs")
+        w1cs = held([P, COLD * PASSES, H], U8, "w1cs")
+        w2hs = held([P, HOT, N], U8, "w2hs")
+        w2cs = held([P, COLD, N], U8, "w2cs")
+        shifted = [held([P, COLD * C], U8, f"shifted{s}") for s in range(1, PASSES)]
+        w1h = [[held([P, 4 * H], U8, f"w1h{e}_{s}") for s in range(PASSES)] for e in range(HOT)]
+        w1c = [held([P, PASSES, 2 * H], U8, f"w1c{f}") for f in range(COLD)]
+        w2h = held([P, HOT, 4 * N], U8, "w2h")
+        w2c = held([P, COLD, 2 * N], U8, "w2c")
+        gate_all = held([P, T], F32, "gate_all")
+        ident = held([P, P], F32, "ident")
+        y_all = held([P, T], F32, "y_all")
+        result = held([P, T], F32, "result")
+        xsg_hot = held([P, HOT * C], U8, "xsg_hot")
+        xsg_cold = held([P, COLD * C], U8, "xsg_cold")
+        xg = {}
+
+        def zero(engine, tile):
+            engine.memset(tile[:].bitcast(I32), 0)
+
+        def load_scale_rows(queue, plane, rows):
+            by_r = rows.bitcast(I32).rearrange("j (q r) w -> r q j w", r=4)
+            for r in range(4):
+                queue.dma_start(out=plane[r:P:32, :, :].bitcast(I32), in_=by_r[r])
+
+        def load_w1h(e, s):
+            nc.sync.dma_start(out=w1h[e][s][:].bitcast(I32),
+                              in_=w1h_words[e, s].rearrange("p i d -> p (i d)").bitcast(I32))
+
+        def load_w1c(f):
+            nc.sync.dma_start(out=w1c[f][:].bitcast(I32),
+                              in_=w1c_words[f].bitcast(I32).rearrange("s p w -> p s w"))
+
+        for tile in (xs, w1cs):
+            zero(nc.vector, tile)
+
+        nc.sync.dma_start(offsets[:], offs)
+        for s in range(PASSES):
+            nc.sync.dma_start(out=xw[s][:], in_=x_words[s].rearrange("p t d -> p (t d)").bitcast(I32))
+        for q in range(4):
+            nc.scalar.dma_start(out=xs[32 * q:32 * q + 4 * PASSES, 0:T].bitcast(I32),
+                                in_=x_scales.bitcast(I32)[:, 4 * q:4 * q + 4, :])
+        load_w1c(7)
+        load_scale_rows(nc.sync, w1cs, w1c_scales.rearrange("f s b i -> (f s) b i"))
+        load_w1c(6)
+        nc.sync.dma_start(out=w2c[:].bitcast(I32),
+                          in_=w2c_words.bitcast(I32).rearrange("f s p w -> p (f s) w"))
+        for f in (5, 4, 3, 2, 1, 0):
+            load_w1c(f)
+        for s in range(PASSES):
+            load_w1h(1, s)
+        nc.sync.dma_start(out=w2h[:].bitcast(I32),
+                          in_=w2h_words.rearrange("e s p n d -> p (e s) (n d)").bitcast(I32))
+        for s in range(PASSES):
+            load_w1h(0, s)
+
+        make_identity(nc, ident[:])
+        for tile in shifted:
+            zero(nc.gpsimd, tile)
+        for plane, rows in ((w2cs, w2c_scales.rearrange("f s b n -> (f s) b n")),
+                            (w1hs, w1h_scales.rearrange("e s b i -> (e s) b i"))):
+            zero(nc.gpsimd, plane)
+            load_scale_rows(nc.gpsimd, plane, rows)
+        nc.gpsimd.dma_start(out=gate_all[:], in_=gate)
+        zero(nc.gpsimd, w2hs)
+        load_scale_rows(nc.gpsimd, w2hs, w2h_scales.rearrange("e s b n -> (e s) b n"))
+
+        def slots(a, b):
+            return offsets[:, a // LIST:b // LIST]
+
+        def gather_words(c, s):
+            xg[c, s] = tokens.tile([P, GATHER], U32, name=f"xg{s}", align_bytes=64)
+            nc.vector.tensor_copy(xg[c, s][:], xw[s][:].bitcast(U32).indirect(slots(c * GATHER, (c + 1) * GATHER)))
+
+        for c in (4, 3, 2):
+            gather_words(c, 0)
+        nc.vector.tensor_copy(xsg_cold[:], xs[:].indirect(slots(HOT * C, T)))
+        for s in range(1, PASSES):
+            nc.scalar.dma_start(out=shifted[s - 1][0:SHIFT_ROWS, :].bitcast(I32),
+                                in_=xsg_cold[4 * s:4 * s + SHIFT_ROWS, :].bitcast(I32))
+        for c in (4, 3, 2, 1, 0):
+            for s in range(PASSES):
+                if (c, s) not in xg:
+                    gather_words(c, s)
+        nc.vector.tensor_copy(xsg_hot[:], xs[:].indirect(slots(0, HOT * C)))
+
+        for e in ORDER:
+            c, u0 = divmod(e * C, GATHER)
+            f = e - HOT
+            pre = psum_h.tile([P, H], F32, name="pre")
+            for s in range(PASSES):
+                if e < HOT:
+                    x_plane = xsg_hot[4 * s:P, e * C:(e + 1) * C]
+                    w = w1h[e][s][:].bitcast(FP8X4)
+                    w_plane = w1hs[:, e * PASSES + s, :]
+                else:
+                    x_plane = ([xsg_cold] + shifted)[s][:, f * C:(f + 1) * C]
+                    w = w1c[f][:, s, :].bitcast(FP4X4)
+                    w_plane = w1cs[:, f * PASSES + s, :]
+                nc.tensor.matmul_mx(out=pre[:], lhsT=xg[c, s][:, u0:u0 + C].bitcast(FP8X4), lhsT_scale=x_plane,
+                                    rhs=w, rhs_scale=w_plane, start=(s == 0), stop=(s == PASSES - 1))
+            relu = ring.tile([P, PACK, P], F32, name="relu", align_bytes=64)
+            nc.scalar.activation(relu[:], pre[:].rearrange("u (m t) -> u t m", t=PACK), ACT.Relu)
+            turned = psum_t.tile([P, PACK, P], F32, name="turned", tag="t")
+            for t in range(PACK):
+                nc.tensor.transpose(turned[:, t, :], relu[:, t, :], ident[:])
+            h = ring.tile([P, C, PACK], BF16, name="h", align_bytes=64)
+            nc.scalar.activation(h[:], turned[:].rearrange("m t u -> m u t"), ACT.Square)
+            h_words = ring.tile([P, C], U32, name="h_words", align_bytes=64)
+            h_plane = ring.tile([P, C], U8, name="h_plane", align_bytes=64)
+            nc.vector.quantize_mx(out=h_words[:].bitcast(FP8X4), scales=h_plane[:],
+                                  in_=h[:].rearrange("m u t -> m (u t)"))
+            y = psum_y.tile([P, C], F32, name="y")
+            if e < HOT:
+                w, w_plane = w2h[:, e, :].bitcast(FP8X4), w2hs[:, e, :]
+            else:
+                w, w_plane = w2c[:, f, :].bitcast(FP4X4), w2cs[:, f, :]
+            nc.tensor.matmul_mx(out=y[:], lhsT=w, lhsT_scale=w_plane, rhs=h_words[:].bitcast(FP8X4),
+                                rhs_scale=h_plane[:], start=True, stop=True)
+            nc.scalar.copy(y_all[:, e * C:(e + 1) * C], y[:])
+            if e in SCATTERS:
+                a, b = SCATTERS[e]
+                nc.vector.tensor_tensor(result[:].indirect(slots(a, b)), y_all[:, a:b], gate_all[:, a:b], MULT)
+
+        nc.sync.dma_start(out=out, in_=result[:])

@@ -26,7 +26,12 @@ SCALE_WINDOW = 1408
 SHIFT_ROWS = 112
 
 ORDER = [9, 8, 7, 6, 5, 4, 3, 2, 1, 0]
+GROUPS = [(0, 8)]
+SCALAR_LOADS = "w2cs w2hs w1hs"
+SYNC_LOADS = "c7 s0 c6 c5 w2c c4 gate c3 c2 c1 c0 h1 w2h h0"
 GATHER = 256
+TURN_LAG = 1
+SECOND_LAG = 2
 SCATTERS = {8: (1120, 1280), 7: (960, 1120), 6: (800, 960), 5: (640, 800), 3: (480, 640), 2: (320, 480), 1: (160, 320), 0: (0, 160)}
 
 
@@ -37,11 +42,11 @@ def tile_moe_hot_mlp_relu2_kernel(
     nc = tc.nc
     with ExitStack() as ctx:
         keep = ctx.enter_context(tc.tile_pool(name="keep", bufs=1))
-        ring = ctx.enter_context(tc.tile_pool(name="ring", bufs=4))
+        ring = ctx.enter_context(tc.tile_pool(name="ring", bufs=6))
         tokens = ctx.enter_context(tc.tile_pool(name="tokens", bufs=5))
-        psum_h = ctx.enter_context(tc.psum_pool(name="psum_h", bufs=3))
+        psum_h = ctx.enter_context(tc.psum_pool(name="psum_h", bufs=2))
         psum_t = ctx.enter_context(tc.psum_pool(name="psum_t", bufs=3))
-        psum_y = ctx.enter_context(tc.psum_pool(name="psum_y", bufs=2))
+        psum_y = ctx.enter_context(tc.psum_pool(name="psum_y", bufs=3))
 
         def held(shape, dtype, name):
             return keep.tile(shape, dtype, name=name, align_bytes=64)
@@ -50,11 +55,11 @@ def tile_moe_hot_mlp_relu2_kernel(
         xw = [held([P, T], I32, f"xw{s}") for s in range(PASSES)]
         xs = held([P, SCALE_WINDOW], U8, "xs")
         w1hs = held([P, HOT * PASSES, H], U8, "w1hs")
-        w1cs = held([P, COLD * PASSES, H], U8, "w1cs")
+        w1cs = {f: held([P, (g - f) * PASSES, H], U8, f"w1cs{f}") for f, g in GROUPS}
         w2hs = held([P, HOT, N], U8, "w2hs")
         w2cs = held([P, COLD, N], U8, "w2cs")
         shifted = [held([P, COLD * C], U8, f"shifted{s}") for s in range(1, PASSES)]
-        w1h = [[held([P, 4 * H], U8, f"w1h{e}_{s}") for s in range(PASSES)] for e in range(HOT)]
+        w1h = [held([P, PASSES, 4 * H], U8, f"w1h{e}") for e in range(HOT)]
         w1c = [held([P, PASSES, 2 * H], U8, f"w1c{f}") for f in range(COLD)]
         w2h = held([P, HOT, 4 * N], U8, "w2h")
         w2c = held([P, COLD, 2 * N], U8, "w2c")
@@ -74,16 +79,21 @@ def tile_moe_hot_mlp_relu2_kernel(
             for r in range(4):
                 queue.dma_start(out=plane[r:P:32, :, :].bitcast(I32), in_=by_r[r])
 
-        def load_w1h(e, s):
-            nc.sync.dma_start(out=w1h[e][s][:].bitcast(I32),
-                              in_=w1h_words[e, s].rearrange("p i d -> p (i d)").bitcast(I32))
+        def load_w1h(e):
+            nc.sync.dma_start(out=w1h[e][:].bitcast(I32),
+                              in_=w1h_words[e].rearrange("s p i d -> p s (i d)").bitcast(I32))
 
         def load_w1c(f):
             nc.sync.dma_start(out=w1c[f][:].bitcast(I32),
                               in_=w1c_words[f].bitcast(I32).rearrange("s p w -> p s w"))
 
-        for tile in (xs, w1cs):
-            zero(nc.vector, tile)
+        for tile in (xs, w2cs, w2hs):
+            zero(nc.gpsimd, tile)
+        for f, g in GROUPS:
+            zero(nc.vector, w1cs[f])
+        make_identity(nc, ident[:])
+        for tile in (shifted[0], shifted[1], w1hs):
+            zero(nc.gpsimd, tile)
 
         nc.sync.dma_start(offsets[:], offs)
         for s in range(PASSES):
@@ -91,30 +101,35 @@ def tile_moe_hot_mlp_relu2_kernel(
         for q in range(4):
             nc.scalar.dma_start(out=xs[32 * q:32 * q + 4 * PASSES, 0:T].bitcast(I32),
                                 in_=x_scales.bitcast(I32)[:, 4 * q:4 * q + 4, :])
-        load_w1c(7)
-        load_scale_rows(nc.sync, w1cs, w1c_scales.rearrange("f s b i -> (f s) b i"))
-        load_w1c(6)
-        nc.sync.dma_start(out=w2c[:].bitcast(I32),
-                          in_=w2c_words.bitcast(I32).rearrange("f s p w -> p (f s) w"))
-        for f in (5, 4, 3, 2, 1, 0):
-            load_w1c(f)
-        for s in range(PASSES):
-            load_w1h(1, s)
-        nc.sync.dma_start(out=w2h[:].bitcast(I32),
-                          in_=w2h_words.rearrange("e s p n d -> p (e s) (n d)").bitcast(I32))
-        for s in range(PASSES):
-            load_w1h(0, s)
+        cold_rows = w1c_scales.rearrange("f s b i -> (f s) b i")
 
-        make_identity(nc, ident[:])
-        for tile in shifted:
-            zero(nc.gpsimd, tile)
-        for plane, rows in ((w2cs, w2c_scales.rearrange("f s b n -> (f s) b n")),
-                            (w1hs, w1h_scales.rearrange("e s b i -> (e s) b i"))):
-            zero(nc.gpsimd, plane)
-            load_scale_rows(nc.gpsimd, plane, rows)
-        nc.gpsimd.dma_start(out=gate_all[:], in_=gate)
-        zero(nc.gpsimd, w2hs)
-        load_scale_rows(nc.gpsimd, w2hs, w2h_scales.rearrange("e s b n -> (e s) b n"))
+        def load(queue, what):
+            if what == "w2cs":
+                load_scale_rows(queue, w2cs, w2c_scales.rearrange("f s b n -> (f s) b n"))
+            elif what == "w2hs":
+                load_scale_rows(queue, w2hs, w2h_scales.rearrange("e s b n -> (e s) b n"))
+            elif what == "w1hs":
+                load_scale_rows(queue, w1hs, w1h_scales.rearrange("e s b i -> (e s) b i"))
+            elif what == "w2c":
+                queue.dma_start(out=w2c[:].bitcast(I32),
+                                in_=w2c_words.bitcast(I32).rearrange("f s p w -> p (f s) w"))
+            elif what == "w2h":
+                queue.dma_start(out=w2h[:].bitcast(I32),
+                                in_=w2h_words.rearrange("e s p n d -> p (e s) (n d)").bitcast(I32))
+            elif what == "gate":
+                queue.dma_start(out=gate_all[:], in_=gate)
+            elif what[0] == "s":
+                f, g = GROUPS[int(what[1])]
+                load_scale_rows(queue, w1cs[f], cold_rows[f * PASSES:g * PASSES])
+            elif what[0] == "c":
+                load_w1c(int(what[1]))
+            else:
+                load_w1h(int(what[1]))
+
+        for what in SCALAR_LOADS.split():
+            load(nc.scalar, what)
+        for what in SYNC_LOADS.split():
+            load(nc.sync, what)
 
         def slots(a, b):
             return offsets[:, a // LIST:b // LIST]
@@ -135,32 +150,44 @@ def tile_moe_hot_mlp_relu2_kernel(
                     gather_words(c, s)
         nc.vector.tensor_copy(xsg_hot[:], xs[:].indirect(slots(0, HOT * C)))
 
-        for e in ORDER:
+        relus, quantised = {}, {}
+
+        def first_layer(e):
             c, u0 = divmod(e * C, GATHER)
             f = e - HOT
             pre = psum_h.tile([P, H], F32, name="pre")
             for s in range(PASSES):
                 if e < HOT:
                     x_plane = xsg_hot[4 * s:P, e * C:(e + 1) * C]
-                    w = w1h[e][s][:].bitcast(FP8X4)
+                    w = w1h[e][:, s, :].bitcast(FP8X4)
                     w_plane = w1hs[:, e * PASSES + s, :]
                 else:
                     x_plane = ([xsg_cold] + shifted)[s][:, f * C:(f + 1) * C]
                     w = w1c[f][:, s, :].bitcast(FP4X4)
-                    w_plane = w1cs[:, f * PASSES + s, :]
+                    first = max(a for a, b in GROUPS if a <= f)
+                    w_plane = w1cs[first][:, (f - first) * PASSES + s, :]
                 nc.tensor.matmul_mx(out=pre[:], lhsT=xg[c, s][:, u0:u0 + C].bitcast(FP8X4), lhsT_scale=x_plane,
                                     rhs=w, rhs_scale=w_plane, start=(s == 0), stop=(s == PASSES - 1))
-            relu = ring.tile([P, PACK, P], F32, name="relu", align_bytes=64)
-            nc.scalar.activation(relu[:], pre[:].rearrange("u (m t) -> u t m", t=PACK), ACT.Relu)
-            turned = psum_t.tile([P, PACK, P], F32, name="turned", tag="t")
+            relus[e] = ring.tile([P, PACK, P], F32, name="relu", align_bytes=64)
+            nc.scalar.activation(relus[e][:], pre[:].rearrange("u (m t) -> u t m", t=PACK), ACT.Relu)
+
+        def turn(k):
+            e = ORDER[k]
+            turned = psum_t.tile([P, PACK, P], F32, name="turned")
             for t in range(PACK):
-                nc.tensor.transpose(turned[:, t, :], relu[:, t, :], ident[:])
+                nc.tensor.transpose(turned[:, t, :], relus[e][:, t, :], ident[:])
             h = ring.tile([P, C, PACK], BF16, name="h", align_bytes=64)
             nc.scalar.activation(h[:], turned[:].rearrange("m t u -> m u t"), ACT.Square)
             h_words = ring.tile([P, C], U32, name="h_words", align_bytes=64)
             h_plane = ring.tile([P, C], U8, name="h_plane", align_bytes=64)
             nc.vector.quantize_mx(out=h_words[:].bitcast(FP8X4), scales=h_plane[:],
                                   in_=h[:].rearrange("m u t -> m (u t)"))
+            quantised[e] = (h_words, h_plane)
+
+        def second_layer(k):
+            e = ORDER[k]
+            f = e - HOT
+            h_words, h_plane = quantised[e]
             y = psum_y.tile([P, C], F32, name="y")
             if e < HOT:
                 w, w_plane = w2h[:, e, :].bitcast(FP8X4), w2hs[:, e, :]
@@ -172,5 +199,13 @@ def tile_moe_hot_mlp_relu2_kernel(
             if e in SCATTERS:
                 a, b = SCATTERS[e]
                 nc.vector.tensor_tensor(result[:].indirect(slots(a, b)), y_all[:, a:b], gate_all[:, a:b], MULT)
+
+        for k in range(E + SECOND_LAG):
+            if k < E:
+                first_layer(ORDER[k])
+            if 0 <= k - TURN_LAG < E:
+                turn(k - TURN_LAG)
+            if 0 <= k - SECOND_LAG < E:
+                second_layer(k - SECOND_LAG)
 
         nc.sync.dma_start(out=out, in_=result[:])

@@ -25,14 +25,11 @@ LIST = 16
 SCALE_WINDOW = 1408
 SHIFT_ROWS = 112
 
-ORDER = [9, 8, 7, 6, 5, 4, 3, 2, 1, 0]
-GROUPS = [(0, 8)]
-SCALAR_LOADS = "w2cs w2hs w1hs"
-SYNC_LOADS = "c7 s0 c6 c5 w2c c4 gate c3 c2 c1 c0 h1 w2h h0"
-GATHER = 256
-TURN_LAG = 1
-SECOND_LAG = 2
-SCATTERS = {8: (1120, 1280), 7: (960, 1120), 6: (800, 960), 5: (640, 800), 3: (480, 640), 2: (320, 480), 1: (160, 320), 0: (0, 160)}
+ORDER = list(range(E - 1, -1, -1))
+SCATTER = 160
+TURN_BANKS = 3
+FIRST_PASS_CUT = 896
+LATER_PASS_CUTS = [1280, 1024, 768, 0]
 
 
 def tile_moe_hot_mlp_relu2_kernel(
@@ -42,118 +39,120 @@ def tile_moe_hot_mlp_relu2_kernel(
     nc = tc.nc
     with ExitStack() as ctx:
         keep = ctx.enter_context(tc.tile_pool(name="keep", bufs=1))
-        ring = ctx.enter_context(tc.tile_pool(name="ring", bufs=6))
-        tokens = ctx.enter_context(tc.tile_pool(name="tokens", bufs=5))
+        ring = ctx.enter_context(tc.tile_pool(name="ring", bufs=5))
         psum_h = ctx.enter_context(tc.psum_pool(name="psum_h", bufs=2))
-        psum_t = ctx.enter_context(tc.psum_pool(name="psum_t", bufs=3))
-        psum_y = ctx.enter_context(tc.psum_pool(name="psum_y", bufs=3))
+        banks = ctx.enter_context(tc.psum_pool(name="banks", bufs=1))
 
         def held(shape, dtype, name):
             return keep.tile(shape, dtype, name=name, align_bytes=64)
 
+        def bank(b):
+            return banks.tile([P, PACK, P], F32, name=f"bank{b}")
+
         offsets = keep.tile([P, T // LIST], U16, name="offsets")
-        xw = [held([P, T], I32, f"xw{s}") for s in range(PASSES)]
-        xs = held([P, SCALE_WINDOW], U8, "xs")
+        x_first = held([P, T], I32, "x_first")
+        x_later = held([P, PASSES - 1, T], I32, "x_later")
+        xw = [x_first[:]] + [x_later[:, s, :] for s in range(PASSES - 1)]
+        xs = held([P, SCALE_WINDOW], U8, "xs_then_words")
         w1hs = held([P, HOT * PASSES, H], U8, "w1hs")
-        w1cs = {f: held([P, (g - f) * PASSES, H], U8, f"w1cs{f}") for f, g in GROUPS}
-        w2hs = held([P, HOT, N], U8, "w2hs")
-        w2cs = held([P, COLD, N], U8, "w2cs")
-        shifted = [held([P, COLD * C], U8, f"shifted{s}") for s in range(1, PASSES)]
+        w1cs = held([P, COLD * PASSES, H], U8, "w1cs")
+        w2s = held([P, E, N], U8, "w2s")
+        w2hs, w2cs = w2s[:, 0:HOT, :], w2s[:, HOT:E, :]
+        shifted = held([P, PASSES - 1, COLD * C], U8, "shifted")
         w1h = [held([P, PASSES, 4 * H], U8, f"w1h{e}") for e in range(HOT)]
         w1c = [held([P, PASSES, 2 * H], U8, f"w1c{f}") for f in range(COLD)]
         w2h = held([P, HOT, 4 * N], U8, "w2h")
         w2c = held([P, COLD, 2 * N], U8, "w2c")
+        gate_rows = held([P, C], F32, "gate_rows")
+        gate_cols = held([P, E], F32, "gate_cols")
         gate_all = held([P, T], F32, "gate_all")
         ident = held([P, P], F32, "ident")
         y_all = held([P, T], F32, "y_all")
         result = held([P, T], F32, "result")
         xsg_hot = held([P, HOT * C], U8, "xsg_hot")
         xsg_cold = held([P, COLD * C], U8, "xsg_cold")
-        xg = {}
 
-        def zero(engine, tile):
-            engine.memset(tile[:].bitcast(I32), 0)
-
-        def load_scale_rows(queue, plane, rows):
+        def load_scale_rows(plane, rows):
             by_r = rows.bitcast(I32).rearrange("j (q r) w -> r q j w", r=4)
             for r in range(4):
-                queue.dma_start(out=plane[r:P:32, :, :].bitcast(I32), in_=by_r[r])
+                nc.sync.dma_start(out=plane[r:P:32, :, :].bitcast(I32), in_=by_r[r])
 
-        def load_w1h(e):
-            nc.sync.dma_start(out=w1h[e][:].bitcast(I32),
-                              in_=w1h_words[e].rearrange("s p i d -> p s (i d)").bitcast(I32))
+        def load_first_matrix(e):
+            if e < HOT:
+                nc.sync.dma_start(out=w1h[e][:].bitcast(I32),
+                                  in_=w1h_words[e].rearrange("s p i d -> p s (i d)").bitcast(I32))
+            else:
+                nc.sync.dma_start(out=w1c[e - HOT][:].bitcast(I32),
+                                  in_=w1c_words[e - HOT].bitcast(I32).rearrange("s p w -> p s w"))
 
-        def load_w1c(f):
-            nc.sync.dma_start(out=w1c[f][:].bitcast(I32),
-                              in_=w1c_words[f].bitcast(I32).rearrange("s p w -> p s w"))
-
-        for tile in (xs, w2cs, w2hs):
-            zero(nc.gpsimd, tile)
-        for f, g in GROUPS:
-            zero(nc.vector, w1cs[f])
+        nc.vector.memset(gate_rows[:], 0.0)
+        for tile in (xs, w1hs, w1cs):
+            nc.vector.memset(tile[:].bitcast(I32), 0)
+        for tile in (w2s, shifted):
+            nc.gpsimd.memset(tile[:].bitcast(I32), 0)
         make_identity(nc, ident[:])
-        for tile in (shifted[0], shifted[1], w1hs):
-            zero(nc.gpsimd, tile)
 
         nc.sync.dma_start(offsets[:], offs)
-        for s in range(PASSES):
-            nc.sync.dma_start(out=xw[s][:], in_=x_words[s].rearrange("p t d -> p (t d)").bitcast(I32))
+        x_rows = x_words.rearrange("s p t d -> p s (t d)").bitcast(I32)
+        nc.sync.dma_start(out=x_first[:], in_=x_rows[:, 0, :])
+        nc.sync.dma_start(out=x_later[:], in_=x_rows[:, 1:PASSES, :])
+        nc.scalar.dma_start(out=gate_rows[0:E, :], in_=gate[0:1, :].rearrange("o (e u) -> (o e) u", u=C))
         for q in range(4):
             nc.scalar.dma_start(out=xs[32 * q:32 * q + 4 * PASSES, 0:T].bitcast(I32),
                                 in_=x_scales.bitcast(I32)[:, 4 * q:4 * q + 4, :])
-        cold_rows = w1c_scales.rearrange("f s b i -> (f s) b i")
 
-        def load(queue, what):
-            if what == "w2cs":
-                load_scale_rows(queue, w2cs, w2c_scales.rearrange("f s b n -> (f s) b n"))
-            elif what == "w2hs":
-                load_scale_rows(queue, w2hs, w2h_scales.rearrange("e s b n -> (e s) b n"))
-            elif what == "w1hs":
-                load_scale_rows(queue, w1hs, w1h_scales.rearrange("e s b i -> (e s) b i"))
-            elif what == "w2c":
-                queue.dma_start(out=w2c[:].bitcast(I32),
-                                in_=w2c_words.bitcast(I32).rearrange("f s p w -> p (f s) w"))
-            elif what == "w2h":
-                queue.dma_start(out=w2h[:].bitcast(I32),
-                                in_=w2h_words.rearrange("e s p n d -> p (e s) (n d)").bitcast(I32))
-            elif what == "gate":
-                queue.dma_start(out=gate_all[:], in_=gate)
-            elif what[0] == "s":
-                f, g = GROUPS[int(what[1])]
-                load_scale_rows(queue, w1cs[f], cold_rows[f * PASSES:g * PASSES])
-            elif what[0] == "c":
-                load_w1c(int(what[1]))
-            else:
-                load_w1h(int(what[1]))
+        load_scale_rows(w2cs, w2c_scales.rearrange("f s b n -> (f s) b n"))
+        load_scale_rows(w1hs, w1h_scales.rearrange("e s b i -> (e s) b i"))
+        load_scale_rows(w1cs, w1c_scales.rearrange("f s b i -> (f s) b i"))
 
-        for what in SCALAR_LOADS.split():
-            load(nc.scalar, what)
-        for what in SYNC_LOADS.split():
-            load(nc.sync, what)
+        columns = bank(TURN_BANKS)
+        nc.tensor.transpose(columns[:, 0, :], gate_rows[:], ident[:])
+        nc.scalar.activation(gate_cols[:], columns[:, 0, 0:E], ACT.Copy)
+        for e0 in range(0, E, PACK):
+            count = min(PACK, E - e0)
+            spread = bank(e0 // PACK)
+            for j in range(count):
+                nc.tensor.transpose(spread[:, j, :], gate_cols[:, e0 + j:e0 + j + 1].to_broadcast([P, P]), ident[:])
+            nc.scalar.copy(gate_all[:, e0 * C:(e0 + count) * C],
+                           spread[:, 0:count, :].rearrange("p j u -> p (j u)"))
 
         def slots(a, b):
             return offsets[:, a // LIST:b // LIST]
 
-        def gather_words(c, s):
-            xg[c, s] = tokens.tile([P, GATHER], U32, name=f"xg{s}", align_bytes=64)
-            nc.vector.tensor_copy(xg[c, s][:], xw[s][:].bitcast(U32).indirect(slots(c * GATHER, (c + 1) * GATHER)))
+        gathered = {}
 
-        for c in (4, 3, 2):
-            gather_words(c, 0)
+        def gather_words(s, a, b, name):
+            tile = held([P, b - a], U32, name)
+            nc.vector.tensor_copy(tile[:], xw[s].bitcast(U32).indirect(slots(a, b)))
+            for e in range(a // C, b // C):
+                gathered[e, s] = tile[:, e * C - a:(e + 1) * C - a]
+
+        gather_words(0, FIRST_PASS_CUT, T, "xg0")
         nc.vector.tensor_copy(xsg_cold[:], xs[:].indirect(slots(HOT * C, T)))
         for s in range(1, PASSES):
-            nc.scalar.dma_start(out=shifted[s - 1][0:SHIFT_ROWS, :].bitcast(I32),
-                                in_=xsg_cold[4 * s:4 * s + SHIFT_ROWS, :].bitcast(I32))
-        for c in (4, 3, 2, 1, 0):
-            for s in range(PASSES):
-                if (c, s) not in xg:
-                    gather_words(c, s)
+            nc.sync.dma_start(out=shifted[0:SHIFT_ROWS, s - 1, :].bitcast(I32),
+                              in_=xsg_cold[4 * s:4 * s + SHIFT_ROWS, :].bitcast(I32))
+        for e in (9, 8, 7):
+            load_first_matrix(e)
+        nc.sync.dma_start(out=w2c[:].bitcast(I32), in_=w2c_words.bitcast(I32).rearrange("f s p w -> p (f s) w"))
+        for e in (6, 5, 4, 3, 2):
+            load_first_matrix(e)
+        nc.sync.dma_start(out=w2h[:].bitcast(I32),
+                          in_=w2h_words.rearrange("e s p n d -> p (e s) (n d)").bitcast(I32))
+        for e in (1, 0):
+            load_first_matrix(e)
+        load_scale_rows(w2hs, w2h_scales.rearrange("e s b n -> (e s) b n"))
         nc.vector.tensor_copy(xsg_hot[:], xs[:].indirect(slots(0, HOT * C)))
+        for s in range(1, PASSES):
+            gather_words(s, LATER_PASS_CUTS[1], T, f"xg{s}_first")
+        gather_words(0, 0, FIRST_PASS_CUT, "xs_then_words")
+        for b, a in zip(LATER_PASS_CUTS[1:], LATER_PASS_CUTS[2:]):
+            for s in range(1, PASSES):
+                gather_words(s, a, b, f"xg{s}_{a}")
 
         relus, quantised = {}, {}
 
         def first_layer(e):
-            c, u0 = divmod(e * C, GATHER)
             f = e - HOT
             pre = psum_h.tile([P, H], F32, name="pre")
             for s in range(PASSES):
@@ -162,18 +161,17 @@ def tile_moe_hot_mlp_relu2_kernel(
                     w = w1h[e][:, s, :].bitcast(FP8X4)
                     w_plane = w1hs[:, e * PASSES + s, :]
                 else:
-                    x_plane = ([xsg_cold] + shifted)[s][:, f * C:(f + 1) * C]
+                    x_plane = xsg_cold[:, f * C:(f + 1) * C] if s == 0 else shifted[:, s - 1, f * C:(f + 1) * C]
                     w = w1c[f][:, s, :].bitcast(FP4X4)
-                    first = max(a for a, b in GROUPS if a <= f)
-                    w_plane = w1cs[first][:, (f - first) * PASSES + s, :]
-                nc.tensor.matmul_mx(out=pre[:], lhsT=xg[c, s][:, u0:u0 + C].bitcast(FP8X4), lhsT_scale=x_plane,
+                    w_plane = w1cs[:, f * PASSES + s, :]
+                nc.tensor.matmul_mx(out=pre[:], lhsT=gathered[e, s].bitcast(FP8X4), lhsT_scale=x_plane,
                                     rhs=w, rhs_scale=w_plane, start=(s == 0), stop=(s == PASSES - 1))
             relus[e] = ring.tile([P, PACK, P], F32, name="relu", align_bytes=64)
             nc.scalar.activation(relus[e][:], pre[:].rearrange("u (m t) -> u t m", t=PACK), ACT.Relu)
 
         def turn(k):
             e = ORDER[k]
-            turned = psum_t.tile([P, PACK, P], F32, name="turned")
+            turned = bank(k % TURN_BANKS)
             for t in range(PACK):
                 nc.tensor.transpose(turned[:, t, :], relus[e][:, t, :], ident[:])
             h = ring.tile([P, C, PACK], BF16, name="h", align_bytes=64)
@@ -188,24 +186,25 @@ def tile_moe_hot_mlp_relu2_kernel(
             e = ORDER[k]
             f = e - HOT
             h_words, h_plane = quantised[e]
-            y = psum_y.tile([P, C], F32, name="y")
+            y = bank(TURN_BANKS + k % TURN_BANKS)
             if e < HOT:
                 w, w_plane = w2h[:, e, :].bitcast(FP8X4), w2hs[:, e, :]
             else:
                 w, w_plane = w2c[:, f, :].bitcast(FP4X4), w2cs[:, f, :]
-            nc.tensor.matmul_mx(out=y[:], lhsT=w, lhsT_scale=w_plane, rhs=h_words[:].bitcast(FP8X4),
+            nc.tensor.matmul_mx(out=y[:, 0, :], lhsT=w, lhsT_scale=w_plane, rhs=h_words[:].bitcast(FP8X4),
                                 rhs_scale=h_plane[:], start=True, stop=True)
-            nc.scalar.copy(y_all[:, e * C:(e + 1) * C], y[:])
-            if e in SCATTERS:
-                a, b = SCATTERS[e]
-                nc.vector.tensor_tensor(result[:].indirect(slots(a, b)), y_all[:, a:b], gate_all[:, a:b], MULT)
+            nc.scalar.copy(y_all[:, e * C:(e + 1) * C], y[:, 0, :])
+            for a in range(T - SCATTER, -1, -SCATTER):
+                if e * C <= a < (e + 1) * C:
+                    nc.vector.tensor_tensor(result[:].indirect(slots(a, a + SCATTER)), y_all[:, a:a + SCATTER],
+                                            gate_all[:, a:a + SCATTER], MULT)
 
-        for k in range(E + SECOND_LAG):
+        for k in range(E + 2):
             if k < E:
                 first_layer(ORDER[k])
-            if 0 <= k - TURN_LAG < E:
-                turn(k - TURN_LAG)
-            if 0 <= k - SECOND_LAG < E:
-                second_layer(k - SECOND_LAG)
+            if 0 <= k - 1 < E:
+                turn(k - 1)
+            if k >= 2:
+                second_layer(k - 2)
 
         nc.sync.dma_start(out=out, in_=result[:])

@@ -28,7 +28,7 @@ SHIFT_ROWS = 112
 ORDER = list(range(E - 1, -1, -1))
 SCATTER = 160
 TURN_BANKS = 3
-FIRST_PASS_CUT = 896
+FIRST_PASS_CUT = 384
 LATER_PASS_CUTS = [1280, 1024, 768, 0]
 
 
@@ -59,7 +59,7 @@ def tile_moe_hot_mlp_relu2_kernel(
         w2s = held([P, E, N], U8, "w2s")
         w2hs, w2cs = w2s[:, 0:HOT, :], w2s[:, HOT:E, :]
         shifted = held([P, PASSES - 1, COLD * C], U8, "shifted")
-        w1h = [held([P, PASSES, 4 * H], U8, f"w1h{e}") for e in range(HOT)]
+        w1h = [[held([P, 4 * H], U8, f"w1h{e}_{s}") for s in range(PASSES)] for e in range(HOT)]
         w1c = [held([P, PASSES, 2 * H], U8, f"w1c{f}") for f in range(COLD)]
         w2h = held([P, HOT, 4 * N], U8, "w2h")
         w2c = held([P, COLD, 2 * N], U8, "w2c")
@@ -79,31 +79,31 @@ def tile_moe_hot_mlp_relu2_kernel(
 
         def load_first_matrix(e):
             if e < HOT:
-                nc.sync.dma_start(out=w1h[e][:].bitcast(I32),
-                                  in_=w1h_words[e].rearrange("s p i d -> p s (i d)").bitcast(I32))
+                for s in range(PASSES):
+                    nc.sync.dma_start(out=w1h[e][s][:].bitcast(I32),
+                                      in_=w1h_words[e, s].rearrange("p i d -> p (i d)").bitcast(I32))
             else:
                 nc.sync.dma_start(out=w1c[e - HOT][:].bitcast(I32),
                                   in_=w1c_words[e - HOT].bitcast(I32).rearrange("s p w -> p s w"))
 
+        nc.vector.memset(xs[:].bitcast(I32), 0)
         nc.vector.memset(gate_rows[:], 0.0)
-        for tile in (xs, w1hs, w1cs):
-            nc.vector.memset(tile[:].bitcast(I32), 0)
-        for tile in (w2s, shifted):
-            nc.gpsimd.memset(tile[:].bitcast(I32), 0)
+        nc.vector.memset(w1cs[:].bitcast(I32), 0)
         make_identity(nc, ident[:])
+        for tile in (w1hs, shifted, w2s):
+            nc.gpsimd.memset(tile[:].bitcast(I32), 0)
 
         nc.sync.dma_start(offsets[:], offs)
         x_rows = x_words.rearrange("s p t d -> p s (t d)").bitcast(I32)
         nc.sync.dma_start(out=x_first[:], in_=x_rows[:, 0, :])
         nc.sync.dma_start(out=x_later[:], in_=x_rows[:, 1:PASSES, :])
-        nc.scalar.dma_start(out=gate_rows[0:E, :], in_=gate[0:1, :].rearrange("o (e u) -> (o e) u", u=C))
         for q in range(4):
             nc.scalar.dma_start(out=xs[32 * q:32 * q + 4 * PASSES, 0:T].bitcast(I32),
                                 in_=x_scales.bitcast(I32)[:, 4 * q:4 * q + 4, :])
+        nc.scalar.dma_start(out=gate_rows[0:E, :], in_=gate[0:1, :].rearrange("o (e u) -> (o e) u", u=C))
 
-        load_scale_rows(w2cs, w2c_scales.rearrange("f s b n -> (f s) b n"))
-        load_scale_rows(w1hs, w1h_scales.rearrange("e s b i -> (e s) b i"))
         load_scale_rows(w1cs, w1c_scales.rearrange("f s b i -> (f s) b i"))
+        load_scale_rows(w1hs, w1h_scales.rearrange("e s b i -> (e s) b i"))
 
         columns = bank(TURN_BANKS)
         nc.tensor.transpose(columns[:, 0, :], gate_rows[:], ident[:])
@@ -132,15 +132,14 @@ def tile_moe_hot_mlp_relu2_kernel(
         for s in range(1, PASSES):
             nc.sync.dma_start(out=shifted[0:SHIFT_ROWS, s - 1, :].bitcast(I32),
                               in_=xsg_cold[4 * s:4 * s + SHIFT_ROWS, :].bitcast(I32))
+        load_scale_rows(w2cs, w2c_scales.rearrange("f s b n -> (f s) b n"))
         for e in (9, 8, 7):
             load_first_matrix(e)
         nc.sync.dma_start(out=w2c[:].bitcast(I32), in_=w2c_words.bitcast(I32).rearrange("f s p w -> p (f s) w"))
-        for e in (6, 5, 4, 3, 2):
+        for e in (6, 5, 4, 3, 2, 1, 0):
             load_first_matrix(e)
         nc.sync.dma_start(out=w2h[:].bitcast(I32),
                           in_=w2h_words.rearrange("e s p n d -> p (e s) (n d)").bitcast(I32))
-        for e in (1, 0):
-            load_first_matrix(e)
         load_scale_rows(w2hs, w2h_scales.rearrange("e s b n -> (e s) b n"))
         nc.vector.tensor_copy(xsg_hot[:], xs[:].indirect(slots(0, HOT * C)))
         for s in range(1, PASSES):
@@ -158,7 +157,7 @@ def tile_moe_hot_mlp_relu2_kernel(
             for s in range(PASSES):
                 if e < HOT:
                     x_plane = xsg_hot[4 * s:P, e * C:(e + 1) * C]
-                    w = w1h[e][:, s, :].bitcast(FP8X4)
+                    w = w1h[e][s][:].bitcast(FP8X4)
                     w_plane = w1hs[:, e * PASSES + s, :]
                 else:
                     x_plane = xsg_cold[:, f * C:(f + 1) * C] if s == 0 else shifted[:, s - 1, f * C:(f + 1) * C]

@@ -20,16 +20,21 @@ MULT = mybir.AluOpType.mult
 
 P = 128
 PACK = 4
+QUADRANT = 32
 PASSES = K // (P * PACK)
 LIST = 16
-SCALE_WINDOW = 1408
-SHIFT_ROWS = 112
 
 ORDER = list(range(E - 1, -1, -1))
-SCATTER = 160
+SCATTER = T // 8
+SCALE_WINDOW = T + C
+SHIFT_ROWS = P - 16
+FIRST_PASS_CUT = 3 * C
+LATER_PASS_CUTS = [T, T - 2 * C, T - 4 * C, 0]
+AHEAD = 2
+BEFORE_W2C = 4
+FIRST_BANKS = 2
 TURN_BANKS = 3
-FIRST_PASS_CUT = 384
-LATER_PASS_CUTS = [1280, 1024, 768, 0]
+RING = BEFORE_W2C + 1
 
 
 def tile_moe_hot_mlp_relu2_kernel(
@@ -39,25 +44,27 @@ def tile_moe_hot_mlp_relu2_kernel(
     nc = tc.nc
     with ExitStack() as ctx:
         keep = ctx.enter_context(tc.tile_pool(name="keep", bufs=1))
-        ring = ctx.enter_context(tc.tile_pool(name="ring", bufs=5))
-        psum_h = ctx.enter_context(tc.psum_pool(name="psum_h", bufs=2))
+        ring = ctx.enter_context(tc.tile_pool(name="ring", bufs=RING))
+        psum_first = ctx.enter_context(tc.psum_pool(name="psum_first", bufs=FIRST_BANKS))
         banks = ctx.enter_context(tc.psum_pool(name="banks", bufs=1))
 
         def held(shape, dtype, name):
             return keep.tile(shape, dtype, name=name, align_bytes=64)
 
-        def bank(b):
-            return banks.tile([P, PACK, P], F32, name=f"bank{b}")
+        def turn_bank(k):
+            return banks.tile([P, PACK, P], F32, name=f"turn_bank{k % TURN_BANKS}")
+
+        def y_bank(k):
+            return banks.tile([P, PACK, P], F32, name=f"y_bank{k % TURN_BANKS}")
 
         offsets = keep.tile([P, T // LIST], U16, name="offsets")
         x_first = held([P, T], I32, "x_first")
         x_later = held([P, PASSES - 1, T], I32, "x_later")
-        xw = [x_first[:]] + [x_later[:, s, :] for s in range(PASSES - 1)]
-        xs = held([P, SCALE_WINDOW], U8, "xs_then_words")
-        w1hs = held([P, HOT * PASSES, H], U8, "w1hs")
-        w1cs = held([P, COLD * PASSES, H], U8, "w1cs")
-        w2s = held([P, E, N], U8, "w2s")
-        w2hs, w2cs = w2s[:, 0:HOT, :], w2s[:, HOT:E, :]
+        x_windows = [x_first[:]] + [x_later[:, s, :] for s in range(PASSES - 1)]
+        x_planes = held([P, SCALE_WINDOW], U8, "planes_then_words")
+        w1h_planes = held([P, HOT * PASSES, H], U8, "w1h_planes")
+        w1c_planes = held([P, COLD * PASSES, H], U8, "w1c_planes")
+        w2_planes = held([P, E, N], U8, "w2_planes")
         shifted = held([P, PASSES - 1, COLD * C], U8, "shifted")
         w1h = [[held([P, 4 * H], U8, f"w1h{e}_{s}") for s in range(PASSES)] for e in range(HOT)]
         w1c = [held([P, PASSES, 2 * H], U8, f"w1c{f}") for f in range(COLD)]
@@ -69,48 +76,49 @@ def tile_moe_hot_mlp_relu2_kernel(
         ident = held([P, P], F32, "ident")
         y_all = held([P, T], F32, "y_all")
         result = held([P, T], F32, "result")
-        xsg_hot = held([P, HOT * C], U8, "xsg_hot")
-        xsg_cold = held([P, COLD * C], U8, "xsg_cold")
+        hot_planes = held([P, HOT * C], U8, "hot_planes")
+        cold_planes = held([P, COLD * C], U8, "cold_planes")
 
-        def load_scale_rows(plane, rows):
-            by_r = rows.bitcast(I32).rearrange("j (q r) w -> r q j w", r=4)
-            for r in range(4):
-                nc.sync.dma_start(out=plane[r:P:32, :, :].bitcast(I32), in_=by_r[r])
+        def load_scale_rows(planes, rows):
+            by_r = rows.bitcast(I32).rearrange("j (q r) w -> r q j w", r=PACK)
+            for r in range(PACK):
+                nc.sync.dma_start(out=planes[r:P:QUADRANT, :, :].bitcast(I32), in_=by_r[r])
 
-        def load_first_matrix(e):
-            if e < HOT:
-                for s in range(PASSES):
-                    nc.sync.dma_start(out=w1h[e][s][:].bitcast(I32),
-                                      in_=w1h_words[e, s].rearrange("p i d -> p (i d)").bitcast(I32))
-            else:
-                nc.sync.dma_start(out=w1c[e - HOT][:].bitcast(I32),
-                                  in_=w1c_words[e - HOT].bitcast(I32).rearrange("s p w -> p s w"))
+        def load_first_matrices(experts):
+            for e in experts:
+                if e < HOT:
+                    for s in range(PASSES):
+                        nc.sync.dma_start(out=w1h[e][s][:].bitcast(I32),
+                                          in_=w1h_words[e, s].rearrange("p i d -> p (i d)").bitcast(I32))
+                else:
+                    nc.sync.dma_start(out=w1c[e - HOT][:].bitcast(I32),
+                                      in_=w1c_words[e - HOT].bitcast(I32).rearrange("s p w -> p s w"))
 
-        nc.vector.memset(xs[:].bitcast(I32), 0)
+        nc.vector.memset(x_planes[:].bitcast(I32), 0)
         nc.vector.memset(gate_rows[:], 0.0)
-        nc.vector.memset(w1cs[:].bitcast(I32), 0)
+        nc.vector.memset(w1c_planes[:].bitcast(I32), 0)
         make_identity(nc, ident[:])
-        for tile in (w1hs, shifted, w2s):
+        for tile in (shifted, w1h_planes, w2_planes):
             nc.gpsimd.memset(tile[:].bitcast(I32), 0)
 
         nc.sync.dma_start(offsets[:], offs)
         x_rows = x_words.rearrange("s p t d -> p s (t d)").bitcast(I32)
         nc.sync.dma_start(out=x_first[:], in_=x_rows[:, 0, :])
         nc.sync.dma_start(out=x_later[:], in_=x_rows[:, 1:PASSES, :])
-        for q in range(4):
-            nc.scalar.dma_start(out=xs[32 * q:32 * q + 4 * PASSES, 0:T].bitcast(I32),
-                                in_=x_scales.bitcast(I32)[:, 4 * q:4 * q + 4, :])
+        for q in range(P // QUADRANT):
+            nc.scalar.dma_start(out=x_planes[QUADRANT * q:QUADRANT * q + PACK * PASSES, 0:T].bitcast(I32),
+                                in_=x_scales.bitcast(I32)[:, PACK * q:PACK * (q + 1), :])
         nc.scalar.dma_start(out=gate_rows[0:E, :], in_=gate[0:1, :].rearrange("o (e u) -> (o e) u", u=C))
 
-        load_scale_rows(w1cs, w1c_scales.rearrange("f s b i -> (f s) b i"))
-        load_scale_rows(w1hs, w1h_scales.rearrange("e s b i -> (e s) b i"))
+        load_first_matrices(ORDER[:AHEAD])
+        load_scale_rows(w1c_planes, w1c_scales.rearrange("f s b i -> (f s) b i"))
 
-        columns = bank(TURN_BANKS)
+        columns = y_bank(0)
         nc.tensor.transpose(columns[:, 0, :], gate_rows[:], ident[:])
         nc.scalar.activation(gate_cols[:], columns[:, 0, 0:E], ACT.Copy)
         for e0 in range(0, E, PACK):
             count = min(PACK, E - e0)
-            spread = bank(e0 // PACK)
+            spread = turn_bank(e0 // PACK)
             for j in range(count):
                 nc.tensor.transpose(spread[:, j, :], gate_cols[:, e0 + j:e0 + j + 1].to_broadcast([P, P]), ident[:])
             nc.scalar.copy(gate_all[:, e0 * C:(e0 + count) * C],
@@ -123,85 +131,81 @@ def tile_moe_hot_mlp_relu2_kernel(
 
         def gather_words(s, a, b, name):
             tile = held([P, b - a], U32, name)
-            nc.vector.tensor_copy(tile[:], xw[s].bitcast(U32).indirect(slots(a, b)))
+            nc.vector.tensor_copy(tile[:], x_windows[s].bitcast(U32).indirect(slots(a, b)))
             for e in range(a // C, b // C):
                 gathered[e, s] = tile[:, e * C - a:(e + 1) * C - a]
 
-        gather_words(0, FIRST_PASS_CUT, T, "xg0")
-        nc.vector.tensor_copy(xsg_cold[:], xs[:].indirect(slots(HOT * C, T)))
+        gather_words(0, FIRST_PASS_CUT, T, "words0_upper")
+        nc.vector.tensor_copy(cold_planes[:], x_planes[:].indirect(slots(HOT * C, T)))
         for s in range(1, PASSES):
             nc.sync.dma_start(out=shifted[0:SHIFT_ROWS, s - 1, :].bitcast(I32),
-                              in_=xsg_cold[4 * s:4 * s + SHIFT_ROWS, :].bitcast(I32))
-        load_scale_rows(w2cs, w2c_scales.rearrange("f s b n -> (f s) b n"))
-        for e in (9, 8, 7):
-            load_first_matrix(e)
+                              in_=cold_planes[PACK * s:PACK * s + SHIFT_ROWS, :].bitcast(I32))
+        load_scale_rows(w1h_planes, w1h_scales.rearrange("e s b i -> (e s) b i"))
+        load_scale_rows(w2_planes[:, HOT:E, :], w2c_scales.rearrange("f s b n -> (f s) b n"))
+        load_first_matrices(ORDER[AHEAD:BEFORE_W2C])
         nc.sync.dma_start(out=w2c[:].bitcast(I32), in_=w2c_words.bitcast(I32).rearrange("f s p w -> p (f s) w"))
-        for e in (6, 5, 4, 3, 2, 1, 0):
-            load_first_matrix(e)
+        load_first_matrices(ORDER[BEFORE_W2C:])
         nc.sync.dma_start(out=w2h[:].bitcast(I32),
                           in_=w2h_words.rearrange("e s p n d -> p (e s) (n d)").bitcast(I32))
-        load_scale_rows(w2hs, w2h_scales.rearrange("e s b n -> (e s) b n"))
-        nc.vector.tensor_copy(xsg_hot[:], xs[:].indirect(slots(0, HOT * C)))
+        load_scale_rows(w2_planes[:, 0:HOT, :], w2h_scales.rearrange("e s b n -> (e s) b n"))
+
+        nc.vector.tensor_copy(hot_planes[:], x_planes[:].indirect(slots(0, HOT * C)))
         for s in range(1, PASSES):
-            gather_words(s, LATER_PASS_CUTS[1], T, f"xg{s}_first")
-        gather_words(0, 0, FIRST_PASS_CUT, "xs_then_words")
+            gather_words(s, LATER_PASS_CUTS[1], T, f"words{s}_{LATER_PASS_CUTS[1]}")
+        gather_words(0, 0, FIRST_PASS_CUT, "planes_then_words")
         for b, a in zip(LATER_PASS_CUTS[1:], LATER_PASS_CUTS[2:]):
             for s in range(1, PASSES):
-                gather_words(s, a, b, f"xg{s}_{a}")
+                gather_words(s, a, b, f"words{s}_{a}")
 
         relus, quantised = {}, {}
 
-        def first_layer(e):
+        def first_layer(k):
+            e = ORDER[k]
             f = e - HOT
-            pre = psum_h.tile([P, H], F32, name="pre")
+            pre = psum_first.tile([P, H], F32, name="pre")
             for s in range(PASSES):
                 if e < HOT:
-                    x_plane = xsg_hot[4 * s:P, e * C:(e + 1) * C]
+                    x_plane = hot_planes[PACK * s:P, e * C:(e + 1) * C]
                     w = w1h[e][s][:].bitcast(FP8X4)
-                    w_plane = w1hs[:, e * PASSES + s, :]
+                    w_plane = w1h_planes[:, e * PASSES + s, :]
                 else:
-                    x_plane = xsg_cold[:, f * C:(f + 1) * C] if s == 0 else shifted[:, s - 1, f * C:(f + 1) * C]
+                    x_plane = cold_planes[:, f * C:(f + 1) * C] if s == 0 else shifted[:, s - 1, f * C:(f + 1) * C]
                     w = w1c[f][:, s, :].bitcast(FP4X4)
-                    w_plane = w1cs[:, f * PASSES + s, :]
+                    w_plane = w1c_planes[:, f * PASSES + s, :]
                 nc.tensor.matmul_mx(out=pre[:], lhsT=gathered[e, s].bitcast(FP8X4), lhsT_scale=x_plane,
                                     rhs=w, rhs_scale=w_plane, start=(s == 0), stop=(s == PASSES - 1))
-            relus[e] = ring.tile([P, PACK, P], F32, name="relu", align_bytes=64)
-            nc.scalar.activation(relus[e][:], pre[:].rearrange("u (m t) -> u t m", t=PACK), ACT.Relu)
+            relus[k] = ring.tile([P, PACK, P], F32, name="relu", align_bytes=64)
+            nc.scalar.activation(relus[k][:], pre[:].rearrange("u (m t) -> u t m", t=PACK), ACT.Relu)
 
         def turn(k):
-            e = ORDER[k]
-            turned = bank(k % TURN_BANKS)
+            turned = turn_bank(k)
             for t in range(PACK):
-                nc.tensor.transpose(turned[:, t, :], relus[e][:, t, :], ident[:])
+                nc.tensor.transpose(turned[:, t, :], relus[k][:, t, :], ident[:])
             h = ring.tile([P, C, PACK], BF16, name="h", align_bytes=64)
             nc.scalar.activation(h[:], turned[:].rearrange("m t u -> m u t"), ACT.Square)
             h_words = ring.tile([P, C], U32, name="h_words", align_bytes=64)
             h_plane = ring.tile([P, C], U8, name="h_plane", align_bytes=64)
             nc.vector.quantize_mx(out=h_words[:].bitcast(FP8X4), scales=h_plane[:],
                                   in_=h[:].rearrange("m u t -> m (u t)"))
-            quantised[e] = (h_words, h_plane)
+            quantised[k] = (h_words, h_plane)
 
         def second_layer(k):
             e = ORDER[k]
-            f = e - HOT
-            h_words, h_plane = quantised[e]
-            y = bank(TURN_BANKS + k % TURN_BANKS)
-            if e < HOT:
-                w, w_plane = w2h[:, e, :].bitcast(FP8X4), w2hs[:, e, :]
-            else:
-                w, w_plane = w2c[:, f, :].bitcast(FP4X4), w2cs[:, f, :]
-            nc.tensor.matmul_mx(out=y[:, 0, :], lhsT=w, lhsT_scale=w_plane, rhs=h_words[:].bitcast(FP8X4),
+            h_words, h_plane = quantised[k]
+            y = y_bank(k)
+            w = w2h[:, e, :].bitcast(FP8X4) if e < HOT else w2c[:, e - HOT, :].bitcast(FP4X4)
+            nc.tensor.matmul_mx(out=y[:, 0, :], lhsT=w, lhsT_scale=w2_planes[:, e, :], rhs=h_words[:].bitcast(FP8X4),
                                 rhs_scale=h_plane[:], start=True, stop=True)
             nc.scalar.copy(y_all[:, e * C:(e + 1) * C], y[:, 0, :])
-            for a in range(T - SCATTER, -1, -SCATTER):
-                if e * C <= a < (e + 1) * C:
+            for a in range(0, T, SCATTER):
+                if a // C == e:
                     nc.vector.tensor_tensor(result[:].indirect(slots(a, a + SCATTER)), y_all[:, a:a + SCATTER],
                                             gate_all[:, a:a + SCATTER], MULT)
 
         for k in range(E + 2):
             if k < E:
-                first_layer(ORDER[k])
-            if 0 <= k - 1 < E:
+                first_layer(k)
+            if 1 <= k <= E:
                 turn(k - 1)
             if k >= 2:
                 second_layer(k - 2)

@@ -21,6 +21,7 @@ MULT = mybir.AluOpType.mult
 P = 128
 PACK = 4
 QUADRANT = 32
+QUADRANTS = P // QUADRANT
 PASSES = K // (P * PACK)
 LIST = 16
 
@@ -28,13 +29,17 @@ ORDER = list(range(E - 1, -1, -1))
 SCATTER = T // 8
 SCALE_WINDOW = T + C
 SHIFT_ROWS = P - 16
-FIRST_PASS_CUT = 3 * C
-LATER_PASS_CUTS = [T, T - 2 * C, T - 4 * C, 0]
-AHEAD = 2
-BEFORE_W2C = 4
-FIRST_BANKS = 2
+AHEAD = 3
+BEHIND = COLD - AHEAD
+WORD_CUTS = [T, T - 2 * C, T - 4 * C, HOT * C, 0]
+W2C_CUTS = [COLD, COLD // 2, 1, 0]
+W2C_AFTER = [AHEAD + 2, AHEAD + 4, E]
+LAST_GROUPS = 2
+SUM_BANKS = 4
 TURN_BANKS = 3
-RING = BEFORE_W2C + 1
+LAG = 3
+HELD = 6
+RING = AHEAD + 2
 
 
 def tile_moe_hot_mlp_relu2_kernel(
@@ -45,7 +50,6 @@ def tile_moe_hot_mlp_relu2_kernel(
     with ExitStack() as ctx:
         keep = ctx.enter_context(tc.tile_pool(name="keep", bufs=1))
         ring = ctx.enter_context(tc.tile_pool(name="ring", bufs=RING))
-        psum_first = ctx.enter_context(tc.psum_pool(name="psum_first", bufs=FIRST_BANKS))
         banks = ctx.enter_context(tc.psum_pool(name="banks", bufs=1))
 
         def held(shape, dtype, name):
@@ -54,22 +58,30 @@ def tile_moe_hot_mlp_relu2_kernel(
         def turn_bank(k):
             return banks.tile([P, PACK, P], F32, name=f"turn_bank{k % TURN_BANKS}")
 
-        def y_bank(k):
-            return banks.tile([P, PACK, P], F32, name=f"y_bank{k % TURN_BANKS}")
+        def sum_bank(k):
+            return banks.tile([P, H], F32, name=f"sum_bank{k % SUM_BANKS}")
+
+        def spare_bank():
+            return banks.tile([P, H], F32, name="spare_bank")
+
+        def load_parts(e, s):
+            return LAST_GROUPS if (e, s) == (ORDER[-1], PASSES - 1) else 1
 
         offsets = keep.tile([P, T // LIST], U16, name="offsets")
         x_first = held([P, T], I32, "x_first")
         x_later = held([P, PASSES - 1, T], I32, "x_later")
         x_windows = [x_first[:]] + [x_later[:, s, :] for s in range(PASSES - 1)]
         x_planes = held([P, SCALE_WINDOW], U8, "planes_then_words")
-        w1h_planes = held([P, HOT * PASSES, H], U8, "w1h_planes")
-        w1c_planes = held([P, COLD * PASSES, H], U8, "w1c_planes")
+        ahead_planes = held([P, AHEAD * PASSES, H], U8, "ahead_planes")
+        behind_planes = held([P, BEHIND * PASSES, H], U8, "behind_planes")
         w2_planes = held([P, E, N], U8, "w2_planes")
+        w1h_planes = held([P, HOT * PASSES, H], U8, "w1h_planes")
         shifted = held([P, PASSES - 1, COLD * C], U8, "shifted")
-        w1h = [[held([P, 4 * H], U8, f"w1h{e}_{s}") for s in range(PASSES)] for e in range(HOT)]
+        w1h = [[[held([P, 4 * H // load_parts(e, s)], U8, f"w1h{e}_{s}_{j}") for j in range(load_parts(e, s))]
+                for s in range(PASSES)] for e in range(HOT)]
         w1c = [held([P, PASSES, 2 * H], U8, f"w1c{f}") for f in range(COLD)]
         w2h = held([P, HOT, 4 * N], U8, "w2h")
-        w2c = held([P, COLD, 2 * N], U8, "w2c")
+        w2c = [held([P, b - a, 2 * N], U8, f"w2c{a}") for b, a in zip(W2C_CUTS, W2C_CUTS[1:])]
         gate_rows = held([P, C], F32, "gate_rows")
         gate_cols = held([P, E], F32, "gate_cols")
         gate_all = held([P, T], F32, "gate_all")
@@ -88,34 +100,39 @@ def tile_moe_hot_mlp_relu2_kernel(
             for e in experts:
                 if e < HOT:
                     for s in range(PASSES):
-                        nc.sync.dma_start(out=w1h[e][s][:].bitcast(I32),
-                                          in_=w1h_words[e, s].rearrange("p i d -> p (i d)").bitcast(I32))
+                        words = w1h_words[e, s].rearrange("p i d -> p (i d)").bitcast(I32)
+                        width = H // load_parts(e, s)
+                        for j, tile in enumerate(w1h[e][s]):
+                            nc.sync.dma_start(out=tile[:].bitcast(I32), in_=words[:, j * width:(j + 1) * width])
                 else:
                     nc.sync.dma_start(out=w1c[e - HOT][:].bitcast(I32),
                                       in_=w1c_words[e - HOT].bitcast(I32).rearrange("s p w -> p s w"))
 
-        nc.vector.memset(x_planes[:].bitcast(I32), 0)
-        nc.vector.memset(gate_rows[:], 0.0)
-        nc.vector.memset(w1c_planes[:].bitcast(I32), 0)
+        nc.gpsimd.memset(x_planes[:].bitcast(I32), 0)
+        nc.gpsimd.memset(gate_rows[:], 0.0)
+        nc.vector.memset(ahead_planes[:].bitcast(I32), 0)
         make_identity(nc, ident[:])
-        for tile in (shifted, w1h_planes, w2_planes):
-            nc.gpsimd.memset(tile[:].bitcast(I32), 0)
+        for tile in (shifted, behind_planes, w2_planes):
+            nc.vector.memset(tile[:].bitcast(I32), 0)
+        nc.gpsimd.memset(w1h_planes[:].bitcast(I32), 0)
 
-        nc.sync.dma_start(offsets[:], offs)
         x_rows = x_words.rearrange("s p t d -> p s (t d)").bitcast(I32)
         nc.sync.dma_start(out=x_first[:], in_=x_rows[:, 0, :])
-        nc.sync.dma_start(out=x_later[:], in_=x_rows[:, 1:PASSES, :])
-        for q in range(P // QUADRANT):
-            nc.scalar.dma_start(out=x_planes[QUADRANT * q:QUADRANT * q + PACK * PASSES, 0:T].bitcast(I32),
-                                in_=x_scales.bitcast(I32)[:, PACK * q:PACK * (q + 1), :])
+        for q in range(QUADRANTS):
+            queue = nc.scalar if q < QUADRANTS // 2 else nc.sync
+            queue.dma_start(out=x_planes[QUADRANT * q:QUADRANT * q + PACK * PASSES, 0:T].bitcast(I32),
+                            in_=x_scales.bitcast(I32)[:, PACK * q:PACK * (q + 1), :])
         nc.scalar.dma_start(out=gate_rows[0:E, :], in_=gate[0:1, :].rearrange("o (e u) -> (o e) u", u=C))
+        nc.sync.dma_start(offsets[:], offs)
+        nc.sync.dma_start(out=x_later[:], in_=x_rows[:, 1:PASSES, :])
 
+        cold_rows = w1c_scales.rearrange("f s b i -> (f s) b i")
         load_first_matrices(ORDER[:AHEAD])
-        load_scale_rows(w1c_planes, w1c_scales.rearrange("f s b i -> (f s) b i"))
+        load_scale_rows(ahead_planes, cold_rows[BEHIND * PASSES:])
 
-        columns = y_bank(0)
-        nc.tensor.transpose(columns[:, 0, :], gate_rows[:], ident[:])
-        nc.scalar.activation(gate_cols[:], columns[:, 0, 0:E], ACT.Copy)
+        columns = spare_bank()
+        nc.tensor.transpose(columns[:, 0:P], gate_rows[:], ident[:])
+        nc.scalar.activation(gate_cols[:], columns[:, 0:E], ACT.Copy)
         for e0 in range(0, E, PACK):
             count = min(PACK, E - e0)
             spread = turn_bank(e0 // PACK)
@@ -129,53 +146,65 @@ def tile_moe_hot_mlp_relu2_kernel(
 
         gathered = {}
 
-        def gather_words(s, a, b, name):
+        def gather_words(s, piece, name):
+            b, a = WORD_CUTS[piece], WORD_CUTS[piece + 1]
             tile = held([P, b - a], U32, name)
             nc.vector.tensor_copy(tile[:], x_windows[s].bitcast(U32).indirect(slots(a, b)))
             for e in range(a // C, b // C):
                 gathered[e, s] = tile[:, e * C - a:(e + 1) * C - a]
 
-        gather_words(0, FIRST_PASS_CUT, T, "words0_upper")
+        gather_words(0, 0, "first_pass_words")
         nc.vector.tensor_copy(cold_planes[:], x_planes[:].indirect(slots(HOT * C, T)))
         for s in range(1, PASSES):
             nc.sync.dma_start(out=shifted[0:SHIFT_ROWS, s - 1, :].bitcast(I32),
                               in_=cold_planes[PACK * s:PACK * s + SHIFT_ROWS, :].bitcast(I32))
+        load_scale_rows(behind_planes, cold_rows[:BEHIND * PASSES])
         load_scale_rows(w1h_planes, w1h_scales.rearrange("e s b i -> (e s) b i"))
         load_scale_rows(w2_planes[:, HOT:E, :], w2c_scales.rearrange("f s b n -> (f s) b n"))
-        load_first_matrices(ORDER[AHEAD:BEFORE_W2C])
-        nc.sync.dma_start(out=w2c[:].bitcast(I32), in_=w2c_words.bitcast(I32).rearrange("f s p w -> p (f s) w"))
-        load_first_matrices(ORDER[BEFORE_W2C:])
+        w2c_rows = w2c_words.bitcast(I32).rearrange("f s p w -> p (f s) w")
+        for part, (begin, end) in enumerate(zip([AHEAD] + W2C_AFTER, W2C_AFTER)):
+            load_first_matrices(ORDER[begin:end])
+            nc.sync.dma_start(out=w2c[part][:].bitcast(I32), in_=w2c_rows[:, W2C_CUTS[part + 1]:W2C_CUTS[part], :])
         nc.sync.dma_start(out=w2h[:].bitcast(I32),
                           in_=w2h_words.rearrange("e s p n d -> p (e s) (n d)").bitcast(I32))
         load_scale_rows(w2_planes[:, 0:HOT, :], w2h_scales.rearrange("e s b n -> (e s) b n"))
 
         nc.vector.tensor_copy(hot_planes[:], x_planes[:].indirect(slots(0, HOT * C)))
-        for s in range(1, PASSES):
-            gather_words(s, LATER_PASS_CUTS[1], T, f"words{s}_{LATER_PASS_CUTS[1]}")
-        gather_words(0, 0, FIRST_PASS_CUT, "planes_then_words")
-        for b, a in zip(LATER_PASS_CUTS[1:], LATER_PASS_CUTS[2:]):
+        gather_words(0, 1, "planes_then_words")
+        for piece in range(len(WORD_CUTS) - 1):
             for s in range(1, PASSES):
-                gather_words(s, a, b, f"words{s}_{a}")
+                gather_words(s, piece, f"words{s}_{piece}")
 
         relus, quantised = {}, {}
 
         def first_layer(k):
             e = ORDER[k]
             f = e - HOT
-            pre = psum_first.tile([P, H], F32, name="pre")
+            sums = [sum_bank(k), spare_bank()] if k == E - 1 else [sum_bank(k)]
+            width = H // len(sums)
             for s in range(PASSES):
-                if e < HOT:
-                    x_plane = hot_planes[PACK * s:P, e * C:(e + 1) * C]
-                    w = w1h[e][s][:].bitcast(FP8X4)
-                    w_plane = w1h_planes[:, e * PASSES + s, :]
-                else:
-                    x_plane = cold_planes[:, f * C:(f + 1) * C] if s == 0 else shifted[:, s - 1, f * C:(f + 1) * C]
-                    w = w1c[f][:, s, :].bitcast(FP4X4)
-                    w_plane = w1c_planes[:, f * PASSES + s, :]
-                nc.tensor.matmul_mx(out=pre[:], lhsT=gathered[e, s].bitcast(FP8X4), lhsT_scale=x_plane,
-                                    rhs=w, rhs_scale=w_plane, start=(s == 0), stop=(s == PASSES - 1))
+                for j, pre in enumerate(sums):
+                    cols = slice(j * width, (j + 1) * width)
+                    if e < HOT:
+                        x_plane = hot_planes[PACK * s:P, e * C:(e + 1) * C]
+                        if load_parts(e, s) == 1:
+                            w = w1h[e][s][0][:].bitcast(FP8X4)[:, cols]
+                        else:
+                            w = w1h[e][s][j][:].bitcast(FP8X4)
+                        w_plane = w1h_planes[:, e * PASSES + s, cols]
+                    else:
+                        x_plane = cold_planes[:, f * C:(f + 1) * C] if s == 0 else shifted[:, s - 1, f * C:(f + 1) * C]
+                        w = w1c[f][:, s, :].bitcast(FP4X4)
+                        if f < BEHIND:
+                            w_plane = behind_planes[:, f * PASSES + s, :]
+                        else:
+                            w_plane = ahead_planes[:, (f - BEHIND) * PASSES + s, :]
+                    nc.tensor.matmul_mx(out=pre[:, 0:width], lhsT=gathered[e, s].bitcast(FP8X4), lhsT_scale=x_plane,
+                                        rhs=w, rhs_scale=w_plane, start=(s == 0), stop=(s == PASSES - 1))
             relus[k] = ring.tile([P, PACK, P], F32, name="relu", align_bytes=64)
-            nc.scalar.activation(relus[k][:], pre[:].rearrange("u (m t) -> u t m", t=PACK), ACT.Relu)
+            for j, pre in enumerate(sums):
+                nc.scalar.activation(relus[k][:, :, j * width // PACK:(j + 1) * width // PACK],
+                                     pre[:, 0:width].rearrange("u (m t) -> u t m", t=PACK), ACT.Relu)
 
         def turn(k):
             turned = turn_bank(k)
@@ -192,22 +221,32 @@ def tile_moe_hot_mlp_relu2_kernel(
         def second_layer(k):
             e = ORDER[k]
             h_words, h_plane = quantised[k]
-            y = y_bank(k)
-            w = w2h[:, e, :].bitcast(FP8X4) if e < HOT else w2c[:, e - HOT, :].bitcast(FP4X4)
-            nc.tensor.matmul_mx(out=y[:, 0, :], lhsT=w, lhsT_scale=w2_planes[:, e, :], rhs=h_words[:].bitcast(FP8X4),
+            y = sum_bank(k + LAG - 1 if k < HELD else k)[:, 0:C]
+            if e < HOT:
+                w = w2h[:, e, :].bitcast(FP8X4)
+            else:
+                part = sum(e - HOT < a for a in W2C_CUTS[1:])
+                w = w2c[part][:, e - HOT - W2C_CUTS[part + 1], :].bitcast(FP4X4)
+            nc.tensor.matmul_mx(out=y, lhsT=w, lhsT_scale=w2_planes[:, e, :], rhs=h_words[:].bitcast(FP8X4),
                                 rhs_scale=h_plane[:], start=True, stop=True)
-            nc.scalar.copy(y_all[:, e * C:(e + 1) * C], y[:, 0, :])
+            nc.scalar.copy(y_all[:, e * C:(e + 1) * C], y)
             for a in range(0, T, SCATTER):
                 if a // C == e:
                     nc.vector.tensor_tensor(result[:].indirect(slots(a, a + SCATTER)), y_all[:, a:a + SCATTER],
                                             gate_all[:, a:a + SCATTER], MULT)
 
+        late_first_pass = {1: (2, "first_pass_words"), 3: (3, "planes_then_words")}
+
         for k in range(E + 2):
             if k < E:
                 first_layer(k)
+            if k in late_first_pass:
+                gather_words(0, *late_first_pass[k])
+            if 0 <= k - LAG < HELD:
+                second_layer(k - LAG)
             if 1 <= k <= E:
                 turn(k - 1)
-            if k >= 2:
+            if HELD <= k - 2 < E:
                 second_layer(k - 2)
 
         nc.sync.dma_start(out=out, in_=result[:])

@@ -64,9 +64,6 @@ def tile_moe_hot_mlp_relu2_kernel(
         def spare_bank():
             return banks.tile([P, H], F32, name="spare_bank")
 
-        def load_parts(e, s):
-            return LAST_GROUPS if (e, s) == (ORDER[-1], PASSES - 1) else 1
-
         offsets = keep.tile([P, T // LIST], U16, name="offsets")
         x_first = held([P, T], I32, "x_first")
         x_later = held([P, PASSES - 1, T], I32, "x_later")
@@ -77,9 +74,12 @@ def tile_moe_hot_mlp_relu2_kernel(
         w2_planes = held([P, E, N], U8, "w2_planes")
         w1h_planes = held([P, HOT * PASSES, H], U8, "w1h_planes")
         shifted = held([P, PASSES - 1, COLD * C], U8, "shifted")
-        w1h = [[[held([P, 4 * H // load_parts(e, s)], U8, f"w1h{e}_{s}_{j}") for j in range(load_parts(e, s))]
-                for s in range(PASSES)] for e in range(HOT)]
-        w1c = [held([P, PASSES, 2 * H], U8, f"w1c{f}") for f in range(COLD)]
+        whole_passes = [PASSES - 1 if e == ORDER[-1] else PASSES for e in range(HOT)]
+        w1h = [held([P, whole_passes[e], 4 * H], U8, f"w1h{e}") for e in range(HOT)]
+        last_pass = [held([P, 4 * H // LAST_GROUPS], U8, f"last_pass{j}") for j in range(LAST_GROUPS)]
+        w1c_ahead = held([P, AHEAD * PASSES, 2 * H], U8, "w1c_ahead")
+        w1c = [held([P, PASSES, 2 * H], U8, f"w1c{f}")[:] for f in range(BEHIND)]
+        w1c = w1c + [w1c_ahead[:, j * PASSES:(j + 1) * PASSES, :] for j in range(AHEAD)]
         w2h = held([P, HOT, 4 * N], U8, "w2h")
         w2c = [held([P, b - a, 2 * N], U8, f"w2c{a}") for b, a in zip(W2C_CUTS, W2C_CUTS[1:])]
         gate_rows = held([P, C], F32, "gate_rows")
@@ -99,13 +99,15 @@ def tile_moe_hot_mlp_relu2_kernel(
         def load_first_matrices(experts):
             for e in experts:
                 if e < HOT:
-                    for s in range(PASSES):
-                        words = w1h_words[e, s].rearrange("p i d -> p (i d)").bitcast(I32)
-                        width = H // load_parts(e, s)
-                        for j, tile in enumerate(w1h[e][s]):
-                            nc.sync.dma_start(out=tile[:].bitcast(I32), in_=words[:, j * width:(j + 1) * width])
+                    words = w1h_words[e].rearrange("s p i d -> p s (i d)").bitcast(I32)
+                    nc.sync.dma_start(out=w1h[e][:].bitcast(I32), in_=words[:, 0:whole_passes[e], :])
+                    if e == ORDER[-1]:
+                        width = H // LAST_GROUPS
+                        for j, tile in enumerate(last_pass):
+                            nc.sync.dma_start(out=tile[:].bitcast(I32),
+                                              in_=words[:, PASSES - 1, j * width:(j + 1) * width])
                 else:
-                    nc.sync.dma_start(out=w1c[e - HOT][:].bitcast(I32),
+                    nc.sync.dma_start(out=w1c[e - HOT].bitcast(I32),
                                       in_=w1c_words[e - HOT].bitcast(I32).rearrange("s p w -> p s w"))
 
         nc.gpsimd.memset(x_planes[:].bitcast(I32), 0)
@@ -127,7 +129,8 @@ def tile_moe_hot_mlp_relu2_kernel(
         nc.sync.dma_start(out=x_later[:], in_=x_rows[:, 1:PASSES, :])
 
         cold_rows = w1c_scales.rearrange("f s b i -> (f s) b i")
-        load_first_matrices(ORDER[:AHEAD])
+        nc.sync.dma_start(out=w1c_ahead[:].bitcast(I32),
+                          in_=w1c_words[BEHIND:].bitcast(I32).rearrange("f s p w -> p (f s) w"))
         load_scale_rows(ahead_planes, cold_rows[BEHIND * PASSES:])
 
         columns = spare_bank()
@@ -187,10 +190,10 @@ def tile_moe_hot_mlp_relu2_kernel(
                     cols = slice(j * width, (j + 1) * width)
                     if e < HOT:
                         x_plane = hot_planes[PACK * s:P, e * C:(e + 1) * C]
-                        if load_parts(e, s) == 1:
-                            w = w1h[e][s][0][:].bitcast(FP8X4)[:, cols]
+                        if (k, s) == (E - 1, PASSES - 1):
+                            w = last_pass[j][:].bitcast(FP8X4)
                         else:
-                            w = w1h[e][s][j][:].bitcast(FP8X4)
+                            w = w1h[e][:, s, :].bitcast(FP8X4)[:, cols]
                         w_plane = w1h_planes[:, e * PASSES + s, cols]
                     else:
                         x_plane = cold_planes[:, f * C:(f + 1) * C] if s == 0 else shifted[:, s - 1, f * C:(f + 1) * C]

@@ -91,10 +91,11 @@ def tile_moe_hot_mlp_relu2_kernel(
         hot_planes = held([P, HOT * C], U8, "hot_planes")
         cold_planes = held([P, COLD * C], U8, "cold_planes")
 
-        def load_scale_rows(planes, rows):
-            by_r = rows.bitcast(I32).rearrange("j (q r) w -> r q j w", r=PACK)
+        def load_scale_rows(*planes_and_rows):
             for r in range(PACK):
-                nc.sync.dma_start(out=planes[r:P:QUADRANT, :, :].bitcast(I32), in_=by_r[r])
+                for planes, rows in planes_and_rows:
+                    by_r = rows.bitcast(I32).rearrange("j (q r) w -> r q j w", r=PACK)
+                    nc.sync.dma_start(out=planes[r:P:QUADRANT, :, :].bitcast(I32), in_=by_r[r])
 
         def load_first_matrices(experts):
             for e in experts:
@@ -131,7 +132,7 @@ def tile_moe_hot_mlp_relu2_kernel(
         cold_rows = w1c_scales.rearrange("f s b i -> (f s) b i")
         nc.sync.dma_start(out=w1c_ahead[:].bitcast(I32),
                           in_=w1c_words[BEHIND:].bitcast(I32).rearrange("f s p w -> p (f s) w"))
-        load_scale_rows(ahead_planes, cold_rows[BEHIND * PASSES:])
+        load_scale_rows((ahead_planes, cold_rows[BEHIND * PASSES:]))
 
         columns = spare_bank()
         nc.tensor.transpose(columns[:, 0:P], gate_rows[:], ident[:])
@@ -161,16 +162,16 @@ def tile_moe_hot_mlp_relu2_kernel(
         for s in range(1, PASSES):
             nc.sync.dma_start(out=shifted[0:SHIFT_ROWS, s - 1, :].bitcast(I32),
                               in_=cold_planes[PACK * s:PACK * s + SHIFT_ROWS, :].bitcast(I32))
-        load_scale_rows(behind_planes, cold_rows[:BEHIND * PASSES])
-        load_scale_rows(w1h_planes, w1h_scales.rearrange("e s b i -> (e s) b i"))
-        load_scale_rows(w2_planes[:, HOT:E, :], w2c_scales.rearrange("f s b n -> (f s) b n"))
+        load_scale_rows((behind_planes, cold_rows[:BEHIND * PASSES]),
+                        (w1h_planes, w1h_scales.rearrange("e s b i -> (e s) b i")),
+                        (w2_planes[:, HOT:E, :], w2c_scales.rearrange("f s b n -> (f s) b n")))
         w2c_rows = w2c_words.bitcast(I32).rearrange("f s p w -> p (f s) w")
         for part, (begin, end) in enumerate(zip([AHEAD] + W2C_AFTER, W2C_AFTER)):
             load_first_matrices(ORDER[begin:end])
             nc.sync.dma_start(out=w2c[part][:].bitcast(I32), in_=w2c_rows[:, W2C_CUTS[part + 1]:W2C_CUTS[part], :])
         nc.sync.dma_start(out=w2h[:].bitcast(I32),
                           in_=w2h_words.rearrange("e s p n d -> p (e s) (n d)").bitcast(I32))
-        load_scale_rows(w2_planes[:, 0:HOT, :], w2h_scales.rearrange("e s b n -> (e s) b n"))
+        load_scale_rows((w2_planes[:, 0:HOT, :], w2h_scales.rearrange("e s b n -> (e s) b n")))
 
         nc.vector.tensor_copy(hot_planes[:], x_planes[:].indirect(slots(0, HOT * C)))
         gather_words(0, 1, "planes_then_words")

@@ -29,11 +29,11 @@ ORDER = list(range(E - 1, -1, -1))
 SCATTER = T // 8
 SCALE_WINDOW = T + C
 SHIFT_ROWS = P - 16
-AHEAD = 3
+AHEAD = 4
 BEHIND = COLD - AHEAD
 WORD_CUTS = [T, T - 2 * C, T - 4 * C, HOT * C, 0]
 W2C_CUTS = [COLD, COLD // 2, 1, 0]
-W2C_AFTER = [AHEAD + 2, AHEAD + 4, E]
+W2C_AFTER = [AHEAD + 1, AHEAD + 3, E]
 LAST_GROUPS = 2
 SUM_BANKS = 4
 TURN_BANKS = 3
@@ -77,9 +77,7 @@ def tile_moe_hot_mlp_relu2_kernel(
         whole_passes = [PASSES - 1 if e == ORDER[-1] else PASSES for e in range(HOT)]
         w1h = [held([P, whole_passes[e], 4 * H], U8, f"w1h{e}") for e in range(HOT)]
         last_pass = [held([P, 4 * H // LAST_GROUPS], U8, f"last_pass{j}") for j in range(LAST_GROUPS)]
-        w1c_ahead = held([P, AHEAD * PASSES, 2 * H], U8, "w1c_ahead")
-        w1c = [held([P, PASSES, 2 * H], U8, f"w1c{f}")[:] for f in range(BEHIND)]
-        w1c = w1c + [w1c_ahead[:, j * PASSES:(j + 1) * PASSES, :] for j in range(AHEAD)]
+        w1c = [held([P, PASSES, 2 * H], U8, f"w1c{f}")[:] for f in range(COLD)]
         w2h = held([P, HOT, 4 * N], U8, "w2h")
         w2c = [held([P, b - a, 2 * N], U8, f"w2c{a}") for b, a in zip(W2C_CUTS, W2C_CUTS[1:])]
         gate_rows = held([P, C], F32, "gate_rows")
@@ -113,25 +111,31 @@ def tile_moe_hot_mlp_relu2_kernel(
 
         nc.gpsimd.memset(x_planes[:].bitcast(I32), 0)
         nc.gpsimd.memset(gate_rows[:], 0.0)
+        nc.vector.memset(w1h_planes[:].bitcast(I32), 0)
         nc.vector.memset(ahead_planes[:].bitcast(I32), 0)
         make_identity(nc, ident[:])
-        for tile in (shifted, behind_planes, w2_planes):
+        for tile in (shifted, w2_planes):
             nc.vector.memset(tile[:].bitcast(I32), 0)
-        nc.gpsimd.memset(w1h_planes[:].bitcast(I32), 0)
 
         x_rows = x_words.rearrange("s p t d -> p s (t d)").bitcast(I32)
+        nc.sync.dma_start(offsets[:], offs)
         nc.sync.dma_start(out=x_first[:], in_=x_rows[:, 0, :])
+        load_first_matrices(ORDER[0:1])
         for q in range(QUADRANTS):
-            queue = nc.scalar if q < QUADRANTS // 2 else nc.sync
+            queue = nc.scalar if q == 0 else nc.sync
             queue.dma_start(out=x_planes[QUADRANT * q:QUADRANT * q + PACK * PASSES, 0:T].bitcast(I32),
                             in_=x_scales.bitcast(I32)[:, PACK * q:PACK * (q + 1), :])
         nc.scalar.dma_start(out=gate_rows[0:E, :], in_=gate[0:1, :].rearrange("o (e u) -> (o e) u", u=C))
-        nc.sync.dma_start(offsets[:], offs)
         nc.sync.dma_start(out=x_later[:], in_=x_rows[:, 1:PASSES, :])
 
+        zeros = w1h_planes[:].rearrange("p j i -> p (j i)").bitcast(U32)
+        later = behind_planes[:].rearrange("p j i -> p (j i)").bitcast(U32)
+        for a in range(0, later.shape[1], zeros.shape[1]):
+            b = min(a + zeros.shape[1], later.shape[1])
+            nc.scalar.copy(later[:, a:b], zeros[:, 0:b - a])
+
         cold_rows = w1c_scales.rearrange("f s b i -> (f s) b i")
-        nc.sync.dma_start(out=w1c_ahead[:].bitcast(I32),
-                          in_=w1c_words[BEHIND:].bitcast(I32).rearrange("f s p w -> p (f s) w"))
+        load_first_matrices(ORDER[1:2])
         load_scale_rows((ahead_planes, cold_rows[BEHIND * PASSES:]))
 
         columns = spare_bank()
@@ -150,22 +154,23 @@ def tile_moe_hot_mlp_relu2_kernel(
 
         gathered = {}
 
-        def gather_words(s, piece, name):
-            b, a = WORD_CUTS[piece], WORD_CUTS[piece + 1]
+        def gather_words(s, b, a, name):
             tile = held([P, b - a], U32, name)
             nc.vector.tensor_copy(tile[:], x_windows[s].bitcast(U32).indirect(slots(a, b)))
             for e in range(a // C, b // C):
                 gathered[e, s] = tile[:, e * C - a:(e + 1) * C - a]
 
-        gather_words(0, 0, "first_pass_words")
+        gather_words(0, T, T - 2 * C, "first_pass_words")
+        gather_words(0, T - 2 * C, T - 4 * C, "second_words")
         nc.vector.tensor_copy(cold_planes[:], x_planes[:].indirect(slots(HOT * C, T)))
         for s in range(1, PASSES):
             nc.sync.dma_start(out=shifted[0:SHIFT_ROWS, s - 1, :].bitcast(I32),
                               in_=cold_planes[PACK * s:PACK * s + SHIFT_ROWS, :].bitcast(I32))
+        w2c_rows = w2c_words.bitcast(I32).rearrange("f s p w -> p (f s) w")
+        load_first_matrices(ORDER[2:AHEAD])
         load_scale_rows((behind_planes, cold_rows[:BEHIND * PASSES]),
                         (w1h_planes, w1h_scales.rearrange("e s b i -> (e s) b i")),
                         (w2_planes[:, HOT:E, :], w2c_scales.rearrange("f s b n -> (f s) b n")))
-        w2c_rows = w2c_words.bitcast(I32).rearrange("f s p w -> p (f s) w")
         for part, (begin, end) in enumerate(zip([AHEAD] + W2C_AFTER, W2C_AFTER)):
             load_first_matrices(ORDER[begin:end])
             nc.sync.dma_start(out=w2c[part][:].bitcast(I32), in_=w2c_rows[:, W2C_CUTS[part + 1]:W2C_CUTS[part], :])
@@ -174,10 +179,10 @@ def tile_moe_hot_mlp_relu2_kernel(
         load_scale_rows((w2_planes[:, 0:HOT, :], w2h_scales.rearrange("e s b n -> (e s) b n")))
 
         nc.vector.tensor_copy(hot_planes[:], x_planes[:].indirect(slots(0, HOT * C)))
-        gather_words(0, 1, "planes_then_words")
-        for piece in range(len(WORD_CUTS) - 1):
+        gather_words(0, HOT * C, 0, "planes_then_words")
+        for b, a in zip(WORD_CUTS, WORD_CUTS[1:]):
             for s in range(1, PASSES):
-                gather_words(s, piece, f"words{s}_{piece}")
+                gather_words(s, b, a, f"words{s}_{a}")
 
         relus, quantised = {}, {}
 
@@ -239,7 +244,7 @@ def tile_moe_hot_mlp_relu2_kernel(
                     nc.vector.tensor_tensor(result[:].indirect(slots(a, a + SCATTER)), y_all[:, a:a + SCATTER],
                                             gate_all[:, a:a + SCATTER], MULT)
 
-        late_first_pass = {1: (2, "first_pass_words"), 3: (3, "planes_then_words")}
+        late_first_pass = {1: (T - 4 * C, HOT * C, "first_pass_words")}
 
         for k in range(E + 2):
             if k < E:

@@ -26,12 +26,12 @@ PASSES = K // (P * PACK)
 LIST = 16
 
 ORDER = list(range(E - 1, -1, -1))
-SCATTER = T // 8
+SCATTER_CUTS = [1280, 1024, 768, 576, 416, 256, 0]
 SCALE_WINDOW = T + C
 SHIFT_ROWS = P - 16
 AHEAD = 4
 BEHIND = COLD - AHEAD
-WORD_CUTS = [T, T - 2 * C, T - 4 * C, HOT * C, 0]
+WORD_CUTS = [T, T - 2 * C, T - 4 * C, 0]
 W2C_CUTS = [COLD, COLD // 2, 1, 0]
 W2C_AFTER = [AHEAD + 1, AHEAD + 3, E]
 LAST_GROUPS = 2
@@ -40,6 +40,8 @@ TURN_BANKS = 3
 LAG = 3
 HELD = 6
 RING = AHEAD + 2
+PAIRED = 4
+HOT_GROUPS = 2
 
 
 def tile_moe_hot_mlp_relu2_kernel(
@@ -72,7 +74,7 @@ def tile_moe_hot_mlp_relu2_kernel(
         ahead_planes = held([P, AHEAD * PASSES, H], U8, "ahead_planes")
         behind_planes = held([P, BEHIND * PASSES, H], U8, "behind_planes")
         w2_planes = held([P, E, N], U8, "w2_planes")
-        w1h_planes = held([P, HOT * PASSES, H], U8, "w1h_planes")
+        w1h_planes = held([P, HOT_GROUPS, H], U8, "w1h_planes")
         shifted = held([P, PASSES - 1, COLD * C], U8, "shifted")
         whole_passes = [PASSES - 1 if e == ORDER[-1] else PASSES for e in range(HOT)]
         w1h = [held([P, whole_passes[e], 4 * H], U8, f"w1h{e}") for e in range(HOT)]
@@ -95,6 +97,16 @@ def tile_moe_hot_mlp_relu2_kernel(
                     by_r = rows.bitcast(I32).rearrange("j (q r) w -> r q j w", r=PACK)
                     nc.sync.dma_start(out=planes[r:P:QUADRANT, :, :].bitcast(I32), in_=by_r[r])
 
+        def load_row(planes, rows, r):
+            by_r = rows.bitcast(I32).rearrange("j (q r) w -> r q j w", r=PACK)
+            nc.sync.dma_start(out=planes[r:P:QUADRANT, :, :].bitcast(I32), in_=by_r[r])
+
+        def load_packed(q, group):
+            rows = w1h_scales.bitcast(I32).rearrange("e s b w -> (e s) b w")
+            planes = rows[PACK * group:min(PACK * (group + 1), HOT * PASSES), PACK * q:PACK * (q + 1), :]
+            nc.sync.dma_start(out=w1h_planes[QUADRANT * q:QUADRANT * q + PACK * planes.shape[0], group, :].bitcast(I32),
+                              in_=planes)
+
         def load_first_matrices(experts):
             for e in experts:
                 if e < HOT:
@@ -111,10 +123,10 @@ def tile_moe_hot_mlp_relu2_kernel(
 
         nc.gpsimd.memset(x_planes[:].bitcast(I32), 0)
         nc.gpsimd.memset(gate_rows[:], 0.0)
-        nc.vector.memset(w1h_planes[:].bitcast(I32), 0)
+        nc.vector.memset(shifted[:].bitcast(I32), 0)
         nc.vector.memset(ahead_planes[:].bitcast(I32), 0)
         make_identity(nc, ident[:])
-        for tile in (shifted, w2_planes):
+        for tile in (w1h_planes, w2_planes):
             nc.vector.memset(tile[:].bitcast(I32), 0)
 
         x_rows = x_words.rearrange("s p t d -> p s (t d)").bitcast(I32)
@@ -128,7 +140,7 @@ def tile_moe_hot_mlp_relu2_kernel(
         nc.scalar.dma_start(out=gate_rows[0:E, :], in_=gate[0:1, :].rearrange("o (e u) -> (o e) u", u=C))
         nc.sync.dma_start(out=x_later[:], in_=x_rows[:, 1:PASSES, :])
 
-        zeros = w1h_planes[:].rearrange("p j i -> p (j i)").bitcast(U32)
+        zeros = shifted[:].rearrange("p j i -> p (j i)").bitcast(U32)
         later = behind_planes[:].rearrange("p j i -> p (j i)").bitcast(U32)
         for a in range(0, later.shape[1], zeros.shape[1]):
             b = min(a + zeros.shape[1], later.shape[1])
@@ -168,9 +180,21 @@ def tile_moe_hot_mlp_relu2_kernel(
                               in_=cold_planes[PACK * s:PACK * s + SHIFT_ROWS, :].bitcast(I32))
         w2c_rows = w2c_words.bitcast(I32).rearrange("f s p w -> p (f s) w")
         load_first_matrices(ORDER[2:AHEAD])
-        load_scale_rows((behind_planes, cold_rows[:BEHIND * PASSES]),
-                        (w1h_planes, w1h_scales.rearrange("e s b i -> (e s) b i")),
-                        (w2_planes[:, HOT:E, :], w2c_scales.rearrange("f s b n -> (f s) b n")))
+        behind = (behind_planes, cold_rows[:BEHIND * PASSES])
+        staged = held([PACK, COLD * QUADRANTS, N], U8, "staged")
+        nc.sync.dma_start(out=staged[:].bitcast(I32),
+                          in_=w2c_scales.bitcast(I32).rearrange("f s (q r) w -> r (f s q) w", r=PACK))
+        for q in range(QUADRANTS):
+            nc.vector.tensor_copy(w2_planes[QUADRANT * q:QUADRANT * q + PACK, HOT:E, :].bitcast(I32),
+                                  staged[:, q::QUADRANTS, :].bitcast(I32))
+        load_row(*behind, 0)
+        for q in range(QUADRANTS):
+            load_packed(q, 0)
+        load_row(*behind, 1)
+        load_row(*behind, 2)
+        load_row(*behind, 3)
+        for q in range(QUADRANTS):
+            load_packed(q, 1)
         for part, (begin, end) in enumerate(zip([AHEAD] + W2C_AFTER, W2C_AFTER)):
             load_first_matrices(ORDER[begin:end])
             nc.sync.dma_start(out=w2c[part][:].bitcast(I32), in_=w2c_rows[:, W2C_CUTS[part + 1]:W2C_CUTS[part], :])
@@ -179,12 +203,11 @@ def tile_moe_hot_mlp_relu2_kernel(
         load_scale_rows((w2_planes[:, 0:HOT, :], w2h_scales.rearrange("e s b n -> (e s) b n")))
 
         nc.vector.tensor_copy(hot_planes[:], x_planes[:].indirect(slots(0, HOT * C)))
-        gather_words(0, HOT * C, 0, "planes_then_words")
         for b, a in zip(WORD_CUTS, WORD_CUTS[1:]):
             for s in range(1, PASSES):
                 gather_words(s, b, a, f"words{s}_{a}")
 
-        relus, quantised = {}, {}
+        relus, quantised, pairs = {}, {}, {}
 
         def first_layer(k):
             e = ORDER[k]
@@ -200,7 +223,8 @@ def tile_moe_hot_mlp_relu2_kernel(
                             w = last_pass[j][:].bitcast(FP8X4)
                         else:
                             w = w1h[e][:, s, :].bitcast(FP8X4)[:, cols]
-                        w_plane = w1h_planes[:, e * PASSES + s, cols]
+                        group, place = divmod(e * PASSES + s, PACK)
+                        w_plane = w1h_planes[PACK * place:P, group, cols]
                     else:
                         x_plane = cold_planes[:, f * C:(f + 1) * C] if s == 0 else shifted[:, s - 1, f * C:(f + 1) * C]
                         w = w1c[f][:, s, :].bitcast(FP4X4)
@@ -219,13 +243,25 @@ def tile_moe_hot_mlp_relu2_kernel(
             turned = turn_bank(k)
             for t in range(PACK):
                 nc.tensor.transpose(turned[:, t, :], relus[k][:, t, :], ident[:])
+            if k < PAIRED:
+                if k % 2 == 0:
+                    pairs[k // 2] = held([P, 2, C, PACK], BF16, f"h_pair{k}")
+                nc.scalar.activation(pairs[k // 2][:, k % 2], turned[:].rearrange("m t u -> m u t"), ACT.Square)
+                if k % 2 == 1:
+                    words = held([P, 2 * C], U32, f"pair_words{k}")
+                    plane = held([P, 2 * C], U8, f"pair_plane{k}")
+                    nc.vector.quantize_mx(out=words[:].bitcast(FP8X4), scales=plane[:],
+                                          in_=pairs[k // 2][:].rearrange("m j u t -> m (j u t)"))
+                    for j in range(2):
+                        quantised[k - 1 + j] = (words[:, j * C:(j + 1) * C], plane[:, j * C:(j + 1) * C])
+                return
             h = ring.tile([P, C, PACK], BF16, name="h", align_bytes=64)
             nc.scalar.activation(h[:], turned[:].rearrange("m t u -> m u t"), ACT.Square)
             h_words = ring.tile([P, C], U32, name="h_words", align_bytes=64)
             h_plane = ring.tile([P, C], U8, name="h_plane", align_bytes=64)
             nc.vector.quantize_mx(out=h_words[:].bitcast(FP8X4), scales=h_plane[:],
                                   in_=h[:].rearrange("m u t -> m (u t)"))
-            quantised[k] = (h_words, h_plane)
+            quantised[k] = (h_words[:], h_plane[:])
 
         def second_layer(k):
             e = ORDER[k]
@@ -236,15 +272,14 @@ def tile_moe_hot_mlp_relu2_kernel(
             else:
                 part = sum(e - HOT < a for a in W2C_CUTS[1:])
                 w = w2c[part][:, e - HOT - W2C_CUTS[part + 1], :].bitcast(FP4X4)
-            nc.tensor.matmul_mx(out=y, lhsT=w, lhsT_scale=w2_planes[:, e, :], rhs=h_words[:].bitcast(FP8X4),
-                                rhs_scale=h_plane[:], start=True, stop=True)
+            nc.tensor.matmul_mx(out=y, lhsT=w, lhsT_scale=w2_planes[:, e, :], rhs=h_words.bitcast(FP8X4),
+                                rhs_scale=h_plane, start=True, stop=True)
             nc.scalar.copy(y_all[:, e * C:(e + 1) * C], y)
-            for a in range(0, T, SCATTER):
+            for b, a in zip(SCATTER_CUTS, SCATTER_CUTS[1:]):
                 if a // C == e:
-                    nc.vector.tensor_tensor(result[:].indirect(slots(a, a + SCATTER)), y_all[:, a:a + SCATTER],
-                                            gate_all[:, a:a + SCATTER], MULT)
+                    nc.vector.tensor_tensor(result[:].indirect(slots(a, b)), y_all[:, a:b], gate_all[:, a:b], MULT)
 
-        late_first_pass = {1: (T - 4 * C, HOT * C, "first_pass_words")}
+        late_first_pass = {1: (T - 4 * C, 0, "first_pass_words")}
 
         for k in range(E + 2):
             if k < E:

from contextlib import ExitStack

import concourse.mybir as mybir
from concourse.masks import make_identity

K, T, E, C, H, N, HOT = 1536, 1280, 10, 128, 512, 128, 2
COLD = E - HOT
FLOPS = 2 * E * C * (K * H + H * N)

F32 = mybir.dt.float32
BF16 = mybir.dt.bfloat16
I32 = mybir.dt.int32
U32 = mybir.dt.uint32
U16 = mybir.dt.uint16
U8 = mybir.dt.uint8
FP8X4 = mybir.dt.float8_e4m3fn_x4
FP4X4 = mybir.dt.float4_e2m1fn_x4
ACT = mybir.ActivationFunctionType
MULT = mybir.AluOpType.mult

P = 128
PACK = 4
QUADRANT = 32
QUADRANTS = P // QUADRANT
PASSES = K // (P * PACK)
LIST = 16

ORDER = list(range(E - 1, -1, -1))
SCATTER_CUTS = [1280, 1024, 768, 576, 416, 256, 0]
SCALE_WINDOW = T + C
SHIFT_ROWS = P - 16
AHEAD = 4
BEHIND = COLD - AHEAD
WORD_CUTS = [T, T - 2 * C, T - 4 * C, 0]
W2C_CUTS = [COLD, COLD // 2, 1, 0]
W2C_AFTER = [AHEAD + 1, AHEAD + 3, E]
LAST_GROUPS = 2
SUM_BANKS = 4
TURN_BANKS = 3
LAG = 3
HELD = 6
RING = AHEAD + 2
PAIRED = 4
HOT_GROUPS = 2


def tile_moe_hot_mlp_relu2_kernel(
    tc, x_words, x_scales, w1h_words, w1h_scales, w2h_words, w2h_scales,
    w1c_words, w1c_scales, w2c_words, w2c_scales, gate, offs, out,
):
    nc = tc.nc
    with ExitStack() as ctx:
        keep = ctx.enter_context(tc.tile_pool(name="keep", bufs=1))
        ring = ctx.enter_context(tc.tile_pool(name="ring", bufs=RING))
        banks = ctx.enter_context(tc.psum_pool(name="banks", bufs=1))

        def held(shape, dtype, name):
            return keep.tile(shape, dtype, name=name, align_bytes=64)

        def turn_bank(k):
            return banks.tile([P, PACK, P], F32, name=f"turn_bank{k % TURN_BANKS}")

        def sum_bank(k):
            return banks.tile([P, H], F32, name=f"sum_bank{k % SUM_BANKS}")

        def spare_bank():
            return banks.tile([P, H], F32, name="spare_bank")

        offsets = keep.tile([P, T // LIST], U16, name="offsets")
        x_first = held([P, T], I32, "x_first")
        x_later = held([P, PASSES - 1, T], I32, "x_later")
        x_windows = [x_first[:]] + [x_later[:, s, :] for s in range(PASSES - 1)]
        x_planes = held([P, SCALE_WINDOW], U8, "planes_then_words")
        ahead_planes = held([P, AHEAD * PASSES, H], U8, "ahead_planes")
        behind_planes = held([P, BEHIND * PASSES, H], U8, "behind_planes")
        w2_planes = held([P, E, N], U8, "w2_planes")
        w1h_planes = held([P, HOT_GROUPS, H], U8, "w1h_planes")
        shifted = held([P, PASSES - 1, COLD * C], U8, "shifted")
        whole_passes = [PASSES - 1 if e == ORDER[-1] else PASSES for e in range(HOT)]
        w1h = [held([P, whole_passes[e], 4 * H], U8, f"w1h{e}") for e in range(HOT)]
        last_pass = [held([P, 4 * H // LAST_GROUPS], U8, f"last_pass{j}") for j in range(LAST_GROUPS)]
        w1c = [held([P, PASSES, 2 * H], U8, f"w1c{f}")[:] for f in range(COLD)]
        w2h = held([P, HOT, 4 * N], U8, "w2h")
        w2c = [held([P, b - a, 2 * N], U8, f"w2c{a}") for b, a in zip(W2C_CUTS, W2C_CUTS[1:])]
        gate_rows = held([P, C], F32, "gate_rows")
        gate_cols = held([P, E], F32, "gate_cols")
        gate_all = held([P, T], F32, "gate_all")
        ident = held([P, P], F32, "ident")
        y_all = held([P, T], F32, "y_all")
        result = held([P, T], F32, "result")
        hot_planes = held([P, HOT * C], U8, "hot_planes")
        cold_planes = held([P, COLD * C], U8, "cold_planes")

        def load_scale_rows(*planes_and_rows):
            for r in range(PACK):
                for planes, rows in planes_and_rows:
                    by_r = rows.bitcast(I32).rearrange("j (q r) w -> r q j w", r=PACK)
                    nc.sync.dma_start(out=planes[r:P:QUADRANT, :, :].bitcast(I32), in_=by_r[r])

        def load_row(planes, rows, r):
            by_r = rows.bitcast(I32).rearrange("j (q r) w -> r q j w", r=PACK)
            nc.sync.dma_start(out=planes[r:P:QUADRANT, :, :].bitcast(I32), in_=by_r[r])

        def load_packed(q, group):
            rows = w1h_scales.bitcast(I32).rearrange("e s b w -> (e s) b w")
            planes = rows[PACK * group:min(PACK * (group + 1), HOT * PASSES), PACK * q:PACK * (q + 1), :]
            nc.sync.dma_start(out=w1h_planes[QUADRANT * q:QUADRANT * q + PACK * planes.shape[0], group, :].bitcast(I32),
                              in_=planes)

        def load_first_matrices(experts):
            for e in experts:
                if e < HOT:
                    words = w1h_words[e].rearrange("s p i d -> p s (i d)").bitcast(I32)
                    nc.sync.dma_start(out=w1h[e][:].bitcast(I32), in_=words[:, 0:whole_passes[e], :])
                    if e == ORDER[-1]:
                        width = H // LAST_GROUPS
                        for j, tile in enumerate(last_pass):
                            nc.sync.dma_start(out=tile[:].bitcast(I32),
                                              in_=words[:, PASSES - 1, j * width:(j + 1) * width])
                else:
                    nc.sync.dma_start(out=w1c[e - HOT].bitcast(I32),
                                      in_=w1c_words[e - HOT].bitcast(I32).rearrange("s p w -> p s w"))

        nc.gpsimd.memset(x_planes[:].bitcast(I32), 0)
        nc.gpsimd.memset(gate_rows[:], 0.0)
        nc.vector.memset(shifted[:].bitcast(I32), 0)
        nc.vector.memset(ahead_planes[:].bitcast(I32), 0)
        make_identity(nc, ident[:])
        for tile in (w1h_planes, w2_planes):
            nc.vector.memset(tile[:].bitcast(I32), 0)

        x_rows = x_words.rearrange("s p t d -> p s (t d)").bitcast(I32)
        nc.sync.dma_start(offsets[:], offs)
        nc.sync.dma_start(out=x_first[:], in_=x_rows[:, 0, :])
        load_first_matrices(ORDER[0:1])
        for q in range(QUADRANTS):
            queue = nc.scalar if q == 0 else nc.sync
            queue.dma_start(out=x_planes[QUADRANT * q:QUADRANT * q + PACK * PASSES, 0:T].bitcast(I32),
                            in_=x_scales.bitcast(I32)[:, PACK * q:PACK * (q + 1), :])
        nc.scalar.dma_start(out=gate_rows[0:E, :], in_=gate[0:1, :].rearrange("o (e u) -> (o e) u", u=C))
        nc.sync.dma_start(out=x_later[:], in_=x_rows[:, 1:PASSES, :])

        zeros = shifted[:].rearrange("p j i -> p (j i)").bitcast(U32)
        later = behind_planes[:].rearrange("p j i -> p (j i)").bitcast(U32)
        for a in range(0, later.shape[1], zeros.shape[1]):
            b = min(a + zeros.shape[1], later.shape[1])
            nc.scalar.copy(later[:, a:b], zeros[:, 0:b - a])

        cold_rows = w1c_scales.rearrange("f s b i -> (f s) b i")
        load_first_matrices(ORDER[1:2])
        load_scale_rows((ahead_planes, cold_rows[BEHIND * PASSES:]))

        columns = spare_bank()
        nc.tensor.transpose(columns[:, 0:P], gate_rows[:], ident[:])
        nc.scalar.activation(gate_cols[:], columns[:, 0:E], ACT.Copy)
        for e0 in range(0, E, PACK):
            count = min(PACK, E - e0)
            spread = turn_bank(e0 // PACK)
            for j in range(count):
                nc.tensor.transpose(spread[:, j, :], gate_cols[:, e0 + j:e0 + j + 1].to_broadcast([P, P]), ident[:])
            nc.scalar.copy(gate_all[:, e0 * C:(e0 + count) * C],
                           spread[:, 0:count, :].rearrange("p j u -> p (j u)"))

        def slots(a, b):
            return offsets[:, a // LIST:b // LIST]

        gathered = {}

        def gather_words(s, b, a, name):
            tile = held([P, b - a], U32, name)
            nc.vector.tensor_copy(tile[:], x_windows[s].bitcast(U32).indirect(slots(a, b)))
            for e in range(a // C, b // C):
                gathered[e, s] = tile[:, e * C - a:(e + 1) * C - a]

        gather_words(0, T, T - 2 * C, "first_pass_words")
        gather_words(0, T - 2 * C, T - 4 * C, "second_words")
        nc.vector.tensor_copy(cold_planes[:], x_planes[:].indirect(slots(HOT * C, T)))
        for s in range(1, PASSES):
            nc.sync.dma_start(out=shifted[0:SHIFT_ROWS, s - 1, :].bitcast(I32),
                              in_=cold_planes[PACK * s:PACK * s + SHIFT_ROWS, :].bitcast(I32))
        w2c_rows = w2c_words.bitcast(I32).rearrange("f s p w -> p (f s) w")
        load_first_matrices(ORDER[2:AHEAD])
        behind = (behind_planes, cold_rows[:BEHIND * PASSES])
        staged = held([PACK, COLD * QUADRANTS, N], U8, "staged")
        nc.sync.dma_start(out=staged[:].bitcast(I32),
                          in_=w2c_scales.bitcast(I32).rearrange("f s (q r) w -> r (f s q) w", r=PACK))
        for q in range(QUADRANTS):
            nc.vector.tensor_copy(w2_planes[QUADRANT * q:QUADRANT * q + PACK, HOT:E, :].bitcast(I32),
                                  staged[:, q::QUADRANTS, :].bitcast(I32))
        load_row(*behind, 0)
        for q in range(QUADRANTS):
            load_packed(q, 0)
        load_row(*behind, 1)
        load_row(*behind, 2)
        load_row(*behind, 3)
        for q in range(QUADRANTS):
            load_packed(q, 1)
        for part, (begin, end) in enumerate(zip([AHEAD] + W2C_AFTER, W2C_AFTER)):
            load_first_matrices(ORDER[begin:end])
            nc.sync.dma_start(out=w2c[part][:].bitcast(I32), in_=w2c_rows[:, W2C_CUTS[part + 1]:W2C_CUTS[part], :])
        nc.sync.dma_start(out=w2h[:].bitcast(I32),
                          in_=w2h_words.rearrange("e s p n d -> p (e s) (n d)").bitcast(I32))
        load_scale_rows((w2_planes[:, 0:HOT, :], w2h_scales.rearrange("e s b n -> (e s) b n")))

        nc.vector.tensor_copy(hot_planes[:], x_planes[:].indirect(slots(0, HOT * C)))
        for b, a in zip(WORD_CUTS, WORD_CUTS[1:]):
            for s in range(1, PASSES):
                gather_words(s, b, a, f"words{s}_{a}")

        relus, quantised, pairs = {}, {}, {}

        def first_layer(k):
            e = ORDER[k]
            f = e - HOT
            sums = [sum_bank(k), spare_bank()] if k == E - 1 else [sum_bank(k)]
            width = H // len(sums)
            for s in range(PASSES):
                for j, pre in enumerate(sums):
                    cols = slice(j * width, (j + 1) * width)
                    if e < HOT:
                        x_plane = hot_planes[PACK * s:P, e * C:(e + 1) * C]
                        if (k, s) == (E - 1, PASSES - 1):
                            w = last_pass[j][:].bitcast(FP8X4)
                        else:
                            w = w1h[e][:, s, :].bitcast(FP8X4)[:, cols]
                        group, place = divmod(e * PASSES + s, PACK)
                        w_plane = w1h_planes[PACK * place:P, group, cols]
                    else:
                        x_plane = cold_planes[:, f * C:(f + 1) * C] if s == 0 else shifted[:, s - 1, f * C:(f + 1) * C]
                        w = w1c[f][:, s, :].bitcast(FP4X4)
                        if f < BEHIND:
                            w_plane = behind_planes[:, f * PASSES + s, :]
                        else:
                            w_plane = ahead_planes[:, (f - BEHIND) * PASSES + s, :]
                    nc.tensor.matmul_mx(out=pre[:, 0:width], lhsT=gathered[e, s].bitcast(FP8X4), lhsT_scale=x_plane,
                                        rhs=w, rhs_scale=w_plane, start=(s == 0), stop=(s == PASSES - 1))
            relus[k] = ring.tile([P, PACK, P], F32, name="relu", align_bytes=64)
            for j, pre in enumerate(sums):
                nc.scalar.activation(relus[k][:, :, j * width // PACK:(j + 1) * width // PACK],
                                     pre[:, 0:width].rearrange("u (m t) -> u t m", t=PACK), ACT.Relu)

        def turn(k):
            turned = turn_bank(k)
            for t in range(PACK):
                nc.tensor.transpose(turned[:, t, :], relus[k][:, t, :], ident[:])
            if k < PAIRED:
                if k % 2 == 0:
                    pairs[k // 2] = held([P, 2, C, PACK], BF16, f"h_pair{k}")
                nc.scalar.activation(pairs[k // 2][:, k % 2], turned[:].rearrange("m t u -> m u t"), ACT.Square)
                if k % 2 == 1:
                    words = held([P, 2 * C], U32, f"pair_words{k}")
                    plane = held([P, 2 * C], U8, f"pair_plane{k}")
                    nc.vector.quantize_mx(out=words[:].bitcast(FP8X4), scales=plane[:],
                                          in_=pairs[k // 2][:].rearrange("m j u t -> m (j u t)"))
                    for j in range(2):
                        quantised[k - 1 + j] = (words[:, j * C:(j + 1) * C], plane[:, j * C:(j + 1) * C])
                return
            h = ring.tile([P, C, PACK], BF16, name="h", align_bytes=64)
            nc.scalar.activation(h[:], turned[:].rearrange("m t u -> m u t"), ACT.Square)
            h_words = ring.tile([P, C], U32, name="h_words", align_bytes=64)
            h_plane = ring.tile([P, C], U8, name="h_plane", align_bytes=64)
            nc.vector.quantize_mx(out=h_words[:].bitcast(FP8X4), scales=h_plane[:],
                                  in_=h[:].rearrange("m u t -> m (u t)"))
            quantised[k] = (h_words[:], h_plane[:])

        def second_layer(k):
            e = ORDER[k]
            h_words, h_plane = quantised[k]
            y = sum_bank(k + LAG - 1 if k < HELD else k)[:, 0:C]
            if e < HOT:
                w = w2h[:, e, :].bitcast(FP8X4)
            else:
                part = sum(e - HOT < a for a in W2C_CUTS[1:])
                w = w2c[part][:, e - HOT - W2C_CUTS[part + 1], :].bitcast(FP4X4)
            nc.tensor.matmul_mx(out=y, lhsT=w, lhsT_scale=w2_planes[:, e, :], rhs=h_words.bitcast(FP8X4),
                                rhs_scale=h_plane, start=True, stop=True)
            nc.scalar.copy(y_all[:, e * C:(e + 1) * C], y)
            for b, a in zip(SCATTER_CUTS, SCATTER_CUTS[1:]):
                if a // C == e:
                    nc.vector.tensor_tensor(result[:].indirect(slots(a, b)), y_all[:, a:b], gate_all[:, a:b], MULT)

        late_first_pass = {1: (T - 4 * C, 0, "first_pass_words")}

        for k in range(E + 2):
            if k < E:
                first_layer(k)
            if k in late_first_pass:
                gather_words(0, *late_first_pass[k])
            if 0 <= k - LAG < HELD:
                second_layer(k - LAG)
            if 1 <= k <= E:
                turn(k - 1)
            if HELD <= k - 2 < E:
                second_layer(k - 2)

        nc.sync.dma_start(out=out, in_=result[:])
